import numpy as np
import ml_dtypes


def mxq(x, axis, fmt="e4m3"):
    dtype, down = {"e4m3": (ml_dtypes.float8_e4m3fn, 7), "e5m2": (ml_dtypes.float8_e5m2, 14)}[fmt]
    v = np.moveaxis(np.asarray(x, np.float32).astype(ml_dtypes.bfloat16).astype(np.float64), axis, -1)
    blocks = v.reshape(v.shape[:-1] + (-1, 32))
    amax = np.abs(blocks).max(-1, keepdims=True)
    byte = np.maximum(np.where(amax > 0, np.frexp(amax)[1] - 1 + 127, 0) - down, 1)
    scale = np.exp2(byte - 127.0)
    codes = (blocks / scale).astype(np.float32).astype(dtype).astype(np.float64)
    return np.moveaxis((codes * scale).reshape(v.shape), -1, axis)


WIDE = False


def mx_kscale(k):
    if not WIDE:
        return np.ones(k)
    levels = np.array([10, -10, 5, -5, 0])
    if k % 512:
        return np.exp2(np.random.permutation(np.resize(levels, k // 32))).repeat(32)
    a = np.empty((k // 512, 16))
    for p in range(k // 512):
        a[p, :8] = np.random.permutation(np.resize(levels, 8))
        for g in range(8):
            far = levels[np.abs(levels - a[p, g]) >= 10]
            a[p, g + 8] = far[np.random.randint(len(far))]
    return np.exp2(a.ravel()).repeat(32)


BF16 = ml_dtypes.bfloat16


def bf(x):
    return np.asarray(x, np.float32).astype(BF16)


def f64(x):
    return np.asarray(x).astype(np.float64)


T, D, F, R, E = 8192, 512, 128, 128, 4
ER = E * R


def draw0():
    u = mx_kscale(D)
    t = mx_kscale(ER)
    return {"x": bf(np.random.standard_normal((T, D)) * u),
            "w0": bf(np.random.standard_normal((D, F)) / np.sqrt(D) / u[:, None]),
            "wa": bf(np.random.standard_normal((D, R)) / np.sqrt(D) / u[:, None]),
            "c": bf(np.random.standard_normal((E, R))),
            "s": bf((1.0 + 0.1 * np.random.standard_normal(ER)) * t),
            "wb": bf(np.random.standard_normal((ER, F)) / np.sqrt(R) / t[:, None])}


def prototype_gate(a, c):
    diff = a[:, None, :] - c[None, :, :]
    logits = -np.sum(diff * diff, axis=-1) / 16.0
    e = np.exp(logits - logits.max(-1, keepdims=True))
    return e / e.sum(-1, keepdims=True)


def core(x, w0, wa, c, s, wb):
    xq = mxq(f64(x), 1, "e4m3")
    a = xq @ mxq(f64(wa), 0, "e4m3")
    g = prototype_gate(a, f64(c))
    z = (g[:, :, None] * a[:, None, :]).reshape(x.shape[0], wb.shape[0])
    zs = z * f64(s)[None, :]
    low = mxq(zs, 1, "e4m3") @ mxq(f64(wb), 0, "e4m3")
    return (xq @ mxq(f64(w0), 0, "e4m3")) + 1.5 * low


def e4m3fn_bytes(y):
    return np.clip(np.asarray(y, np.float64), -448.0, 448.0).astype(np.float32).astype(ml_dtypes.float8_e4m3fn).view(np.uint8)


def e4m3fn_values(b):
    return np.asarray(b, np.uint8).view(ml_dtypes.float8_e4m3fn).astype(np.float64)


def setup_inputs():
    d = draw0()
    x0 = np.asarray(d['x']).astype(np.float64)
    s = (np.max(np.abs(x0), axis=(0,), keepdims=True) / 448.0).astype(np.float32)
    out = {}
    for k, v in d.items():
        if k == 'x':
            out['x_bytes'] = e4m3fn_bytes(x0 / s.astype(np.float64))
            out['x_scale'] = s
        else:
            out[k] = v
    return out


def reference(x_bytes, x_scale, w0, wa, c, s, wb):
    return core(e4m3fn_values(x_bytes) * x_scale.astype(np.float64), w0, wa, c, s, wb)

@@ -1,0 +1,312 @@
+from contextlib import ExitStack
+
+import concourse.mybir as mybir
+from concourse.masks import make_identity
+
+T, D, F, R, E = 8192, 512, 128, 128, 4
+P = 128
+G = 4
+GT = G * P
+NG = T // GT
+M = T // P
+FLOPS = 2 * T * D * (F + R) + 2 * T * E * R * F
+
+F32 = mybir.dt.float32
+BF16 = mybir.dt.bfloat16
+U32 = mybir.dt.uint32
+U8 = mybir.dt.uint8
+FP8 = mybir.dt.float8_e4m3fn
+FP8X4 = mybir.dt.float8_e4m3fn_x4
+ALU = mybir.AluOpType
+ACT = mybir.ActivationFunctionType
+AX = mybir.AxisListType
+
+
+def tile_hydraloraprototyperouted_t_kernel(tc, x_bytes, x_scale, w0, wa, c, s, wb, out):
+    nc = tc.nc
+    x_view = x_bytes.rearrange("(p m) k -> p m k", m=M)
+    out_view = out.rearrange("(p m) f -> p m f", m=M)
+
+    with ExitStack() as ctx:
+        keep = ctx.enter_context(tc.tile_pool(name="keep", bufs=1))
+        byte_pool = ctx.enter_context(tc.tile_pool(name="byte_pool", bufs=NG))
+        work = ctx.enter_context(tc.tile_pool(name="work", bufs=3))
+        psum = ctx.enter_context(tc.psum_pool(name="psum", bufs=1))
+        ctx.enter_context(tc.manual_schedule())
+
+        ident = keep.tile([P, P], F32, name="ident")
+        make_identity(nc, ident[:])
+
+        scale = keep.tile([P, 2 * D], F32, name="scale")
+        nc.scalar.dma_start(out=scale[:, 0:D], in_=x_scale.rearrange("o k -> (o k)").partition_broadcast(P))
+        xbytes = {}
+
+        def load(g):
+            xbytes[g] = byte_pool.tile([P, G * D], U8, name="xbytes")
+            nc.sync.dma_start(
+                out=xbytes[g][:].rearrange("p (m k) -> p m k", m=G),
+                in_=x_view[:, G * g : G * g + G, :],
+            )
+
+        load(0)
+        raw = {}
+
+        def load_w(nm, ap):
+            raw[nm] = keep.tile([P, 4, P], BF16, name="raw_" + nm)
+            nc.sync.dma_start(out=raw[nm][:], in_=ap.rearrange("(p j) w -> p j w", j=4))
+
+        load_w("wa", wa)
+        load_w("w0", w0)
+        load(1)
+        load_w("wb", wb)
+        cb = keep.tile([P, E * R], BF16, name="cb")
+        nc.scalar.dma_start(out=cb[:], in_=c.rearrange("e r -> (e r)").partition_broadcast(P))
+        sb = keep.tile([P, E * R], BF16, name="sb")
+        nc.scalar.dma_start(out=sb[:], in_=s.partition_broadcast(P))
+        for g in range(2, NG):
+            load(g)
+
+        dummy = keep.tile([P, 1], F32, name="dummy")
+        dummy_out = keep.tile([P, 1], F32, name="dummy_out")
+        nc.vector.memset(dummy[:], 0.0)
+        nc.scalar.activation(out=dummy_out[:], in_=dummy[:], func=ACT.Exp)
+
+        grp_a = keep.tile([P, 2, P, 4], BF16, name="grp_a", align_bytes=64)
+        grp_b = keep.tile([P, 2, P, 4], BF16, name="grp_b", align_bytes=64)
+        wcode_a = keep.tile([P, 2 * P], U32, name="wcode_a", align_bytes=64)
+        wcode_b = keep.tile([P, 2 * P], U32, name="wcode_b", align_bytes=64)
+        wscale_a = keep.tile([P, 2 * P], U8, name="wscale_a", align_bytes=64)
+        wscale_b = keep.tile([P, 2 * P], U8, name="wscale_b", align_bytes=64)
+        for u in range(2):
+            nc.scalar.copy(
+                out=grp_a[:, 0, 64 * u : 64 * u + 64, :].rearrange("p (q i) j -> p q i j", i=2),
+                in_=raw["wa"][:].rearrange("p j (q u i) -> p u q i j", u=2, i=2)[:, u],
+            )
+        nc.scalar.copy(out=scale[:, D : 2 * D], in_=scale[:, 0:D])
+
+        xb, xc, xs = {}, {}, {}
+        xg, zg, zsrc = {}, {}, {}
+        a_ps, o_ps, l_ps = {}, {}, {}
+        at_sb, z1, mn, ex, sm, rc, gt = {}, {}, {}, {}, {}, {}, {}
+
+        def widen(g, lo, hi):
+            if lo == 0:
+                xb[g] = work.tile([P, G * D], BF16, name="xb", align_bytes=64)
+            w = hi - lo
+            nc.vector.tensor_tensor(
+                out=xb[g][:, lo:hi], in0=xbytes[g][:, lo:hi].bitcast(FP8), in1=scale[:, 0:w], op=ALU.mult
+            )
+
+        def turn(src_words, step, dst, half):
+            bank = psum.tile([P, 2, 2, P], F32, name="turned", bufs=3)
+            for jj in range(2):
+                base = 256 * (2 * half + jj)
+                for u in range(2):
+                    if step == 2:
+                        cols = src_words[:, base + u : base + 256 : 2]
+                    else:
+                        cols = src_words[:, base + 128 * u : base + 128 * u + 128]
+                    nc.tensor.transpose(bank[:, jj, u, :], cols, ident[:])
+            nc.scalar.copy(
+                out=dst[:, 1024 * half : 1024 * half + 1024].bitcast(F32).rearrange("p (j n u) -> p j n u", j=2, u=2),
+                in_=bank[:].rearrange("p j u n -> p j n u"),
+            )
+
+        def turn_x(g, half):
+            if half == 0:
+                xg[g] = work.tile([P, 4 * GT], BF16, name="xg", align_bytes=64)
+            turn(xb[g][:].bitcast(F32), 2, xg[g], half)
+
+        def turn_z(g, half):
+            if half == 0:
+                zg[g] = work.tile([P, 4 * GT], BF16, name="zg", align_bytes=64)
+            turn(zsrc[g][:].rearrange("p m k -> p (m k)").bitcast(F32), 1, zg[g], half)
+
+        def quant_x(g):
+            xc[g] = work.tile([P, GT], U32, name="xc", align_bytes=64)
+            xs[g] = work.tile([P, GT], U8, name="xs", align_bytes=64)
+            nc.vector.quantize_mx(out=xc[g][:].bitcast(FP8X4), scales=xs[g][:], in_=xg[g][:])
+
+        zc, zsc = {}, {}
+
+        def quant_z(g):
+            zc[g] = work.tile([P, GT], U32, name="zc", align_bytes=64)
+            zsc[g] = work.tile([P, GT], U8, name="zsc", align_bytes=64)
+            nc.vector.quantize_mx(out=zc[g][:].bitcast(FP8X4), scales=zsc[g][:], in_=zg[g][:])
+
+        def mm(o, lc, ls, rc_, rs, start, stop):
+            nc.tensor.matmul_mx(
+                out=o, lhsT=lc.bitcast(FP8X4), lhsT_scale=ls, rhs=rc_.bitcast(FP8X4), rhs_scale=rs, start=start, stop=stop
+            )
+
+        def project(g):
+            at = psum.tile([P, GT], F32, name="at", bufs=1)
+            mm(at[:], wcode_a[:, 0:P], wscale_a[:, 0:P], xc[g][:], xs[g][:], True, True)
+            a_ps[g] = psum.tile([P, G, R], F32, name="a_ps", bufs=2)
+            for j in range(G):
+                cols = slice(P * j, P * j + P)
+                mm(a_ps[g][:, j, :], xc[g][:, cols], xs[g][:, cols], wcode_a[:, 0:P], wscale_a[:, 0:P], True, True)
+            at_sb[g] = work.tile([P, GT], F32, name="at_sb")
+            nc.scalar.copy(out=at_sb[g][:], in_=at[:])
+
+        def logits(g):
+            l_ps[g] = psum.tile([P, G, E], F32, name="l_ps", bufs=1)
+            for j in range(G):
+                nc.tensor.matmul(
+                    l_ps[g][:, j, :], lhsT=at_sb[g][:, P * j : P * j + P], rhs=ct[:], start=True, stop=True
+                )
+
+        def soft1(g):
+            z1[g] = work.tile([P, G, E], F32, name="z1")
+            nc.vector.scalar_tensor_tensor(
+                out=z1[g][:], in0=l_ps[g][:], scalar=-0.125, in1=csq[:], op0=ALU.mult, op1=ALU.add
+            )
+
+        def soft2(g):
+            mn[g] = work.tile([P, G], F32, name="mn")
+            nc.vector.tensor_reduce(out=mn[g][:], in_=z1[g][:], axis=AX.X, op=ALU.min)
+
+        def soft3(g):
+            ex[g] = work.tile([P, G, E], F32, name="ex")
+            sm[g] = work.tile([P, G], F32, name="sm")
+            for j in range(G):
+                nc.scalar.activation(
+                    out=ex[g][:, j, :], in_=z1[g][:, j, :], func=ACT.Exp, scale=-1.0,
+                    bias=mn[g][:, j : j + 1], accum_out=sm[g][:, j : j + 1],
+                )
+
+        def soft4(g):
+            rc[g] = work.tile([P, G], F32, name="rc")
+            nc.vector.reciprocal(out=rc[g][:], in_=sm[g][:])
+
+        def soft5(g):
+            gt[g] = work.tile([P, G, E], F32, name="gt")
+            nc.vector.tensor_tensor(
+                out=gt[g][:], in0=ex[g][:], in1=rc[g][:].unsqueeze(2).to_broadcast([P, G, E]), op=ALU.mult
+            )
+
+        def mix(g, j):
+            if j == 0:
+                zsrc[g] = work.tile([P, G, E * R], BF16, name="zsrc", align_bytes=64)
+            dst = zsrc[g][:, j, :].rearrange("p (u m) -> p u m", u=2)
+            for e in range(E):
+                nc.vector.scalar_tensor_tensor(
+                    out=dst[:, :, 64 * e : 64 * e + 64],
+                    in0=a_ps[g][:, j, :].rearrange("p (u m) -> p u m", u=2),
+                    scalar=gt[g][:, j, e : e + 1],
+                    in1=sp[:, e, :].rearrange("p (u m) -> p u m", u=2),
+                    op0=ALU.mult,
+                    op1=ALU.mult,
+                )
+
+        def combine(g):
+            o_ps[g] = psum.tile([P, G, F], F32, name="o_ps", bufs=1)
+            for j in range(G):
+                cols = slice(P * j, P * j + P)
+                o = o_ps[g][:, j, :]
+                mm(o, xc[g][:, cols], xs[g][:, cols], wcode_a[:, P : 2 * P], wscale_a[:, P : 2 * P], True, False)
+                mm(o, zc[g][:, cols], zsc[g][:, cols], wcode_b[:, 0:P], wscale_b[:, 0:P], False, False)
+                mm(o, zc[g][:, cols], zsc[g][:, cols], wcode_b[:, P : 2 * P], wscale_b[:, P : 2 * P], False, True)
+
+        def store(g):
+            o_sb = work.tile([P, G, F], F32, name="o_sb")
+            nc.scalar.copy(out=o_sb[:], in_=o_ps[g][:])
+            nc.sync.dma_start(out=out_view[:, G * g : G * g + G, :], in_=o_sb[:])
+
+        widen(0, 0, 512)
+        widen(0, 512, 1024)
+        turn_x(0, 0)
+        nc.scalar.copy(out=grp_a[:, 1], in_=raw["w0"][:].rearrange("p j w -> p w j"))
+        widen(0, 1024, 2048)
+        turn_x(0, 1)
+        nc.vector.quantize_mx(
+            out=wcode_a[:].bitcast(FP8X4), scales=wscale_a[:], in_=grp_a[:].rearrange("p a w j -> p (a w j)")
+        )
+        cp = keep.tile([P, E, R], F32, name="cp")
+        for u in range(2):
+            nc.scalar.copy(
+                out=cp[:, :, 64 * u : 64 * u + 64].rearrange("p e (q i) -> p e q i", i=2),
+                in_=cb[:].rearrange("p (e q u i) -> p u e q i", e=E, u=2, i=2)[:, u],
+            )
+        c_ps = psum.tile([P, E, P], F32, name="turned", bufs=3)
+        for e in range(E):
+            nc.tensor.transpose(c_ps[:, e, :], cp[:, e, :], ident[:])
+        ct = keep.tile([P, E], F32, name="ct")
+        nc.scalar.copy(out=ct[:], in_=c_ps[:, :, 0])
+        csq1 = keep.tile([P, E], F32, name="csq1")
+        cjunk = keep.tile([P, R], F32, name="cjunk")
+        for e in range(E):
+            nc.scalar.activation(
+                out=cjunk[:], in_=cp[:, e, :], func=ACT.Square, scale=0.25, accum_out=csq1[:, e : e + 1]
+            )
+        csq = keep.tile([P, G, E], F32, name="csq")
+        nc.scalar.copy(out=csq[:], in_=csq1[:].unsqueeze(1).to_broadcast([P, G, E]))
+
+        widen(1, 0, 1024)
+        turn_x(1, 0)
+        widen(1, 1024, 2048)
+        turn_x(1, 1)
+        sp = keep.tile([P, E, R], F32, name="sp")
+        for u in range(2):
+            nc.scalar.copy(
+                out=sp[:, :, 64 * u : 64 * u + 64].rearrange("p e (q i) -> p e q i", i=2),
+                in_=sb[:].rearrange("p (e q u i) -> p u e q i", e=E, u=2, i=2)[:, u],
+            )
+        quant_x(0)
+        project(0)
+        logits(0)
+        widen(2, 0, 1024)
+        turn_x(2, 0)
+        soft1(0)
+        widen(2, 1024, 2048)
+        soft2(0)
+        soft3(0)
+        turn_x(2, 1)
+        nc.scalar.copy(out=grp_b[:, 0], in_=raw["wb"][:].rearrange("p j w -> p w j"))
+        nc.scalar.activation(
+            out=grp_b[:, 1], in_=raw["wb"][:].rearrange("p j w -> p w j"), func=ACT.Copy, scale=0.5
+        )
+        soft4(0)
+        soft5(0)
+
+        for k in range(NG):
+            nxt = k + 1 < NG
+            far = k + 3 < NG
+            if nxt:
+                quant_x(k + 1)
+            if k == 0:
+                nc.vector.quantize_mx(
+                    out=wcode_b[:].bitcast(FP8X4), scales=wscale_b[:], in_=grp_b[:].rearrange("p a w j -> p (a w j)")
+                )
+            if k > 0:
+                combine(k - 1)
+            if nxt:
+                project(k + 1)
+            if k > 0:
+                store(k - 1)
+            if nxt:
+                logits(k + 1)
+            mix(k, 0)
+            mix(k, 1)
+            turn_z(k, 0)
+            mix(k, 2)
+            mix(k, 3)
+            turn_z(k, 1)
+            if nxt:
+                soft1(k + 1)
+            if far:
+                widen(k + 3, 0, 1024)
+            if nxt:
+                soft2(k + 1)
+                soft3(k + 1)
+            if far:
+                turn_x(k + 3, 0)
+                widen(k + 3, 1024, 2048)
+                turn_x(k + 3, 1)
+            if nxt:
+                soft4(k + 1)
+            quant_z(k)
+            if nxt:
+                soft5(k + 1)
+        combine(NG - 1)
+        store(NG - 1)

@@ -61,8 +61,8 @@ def tile_hydraloraprototyperouted_t_kernel(tc, x_bytes, x_scale, w0, wa, c, s, w
         load_w("wb", wb)
         cb = keep.tile([P, E * R], BF16, name="cb")
         nc.scalar.dma_start(out=cb[:], in_=c.rearrange("e r -> (e r)").partition_broadcast(P))
-        sb = keep.tile([P, E * R], BF16, name="sb")
-        nc.scalar.dma_start(out=sb[:], in_=s.partition_broadcast(P))
+        s_raw = keep.tile([P, 4], BF16, name="s_raw")
+        nc.scalar.dma_start(out=s_raw[:], in_=s.rearrange("(p t) -> p t", t=4))
         for g in range(2, NG):
             load(g)
 
@@ -73,81 +73,109 @@ def tile_hydraloraprototyperouted_t_kernel(tc, x_bytes, x_scale, w0, wa, c, s, w
 
         grp_a = keep.tile([P, 2, P, 4], BF16, name="grp_a", align_bytes=64)
         grp_b = keep.tile([P, 2, P, 4], BF16, name="grp_b", align_bytes=64)
+        grp_r = keep.tile([P, 4, E, 32, 4], BF16, name="grp_r", align_bytes=64)
         wcode_a = keep.tile([P, 2 * P], U32, name="wcode_a", align_bytes=64)
         wcode_b = keep.tile([P, 2 * P], U32, name="wcode_b", align_bytes=64)
+        wcode_r = keep.tile([P, 4 * P], U32, name="wcode_r", align_bytes=64)
         wscale_a = keep.tile([P, 2 * P], U8, name="wscale_a", align_bytes=64)
         wscale_b = keep.tile([P, 2 * P], U8, name="wscale_b", align_bytes=64)
-        for u in range(2):
-            nc.scalar.copy(
-                out=grp_a[:, 0, 64 * u : 64 * u + 64, :].rearrange("p (q i) j -> p q i j", i=2),
-                in_=raw["wa"][:].rearrange("p j (q u i) -> p u q i j", u=2, i=2)[:, u],
-            )
+        wscale_r = keep.tile([P, 4 * P], U8, name="wscale_r", align_bytes=64)
+        nc.scalar.copy(out=grp_a[:, 0], in_=raw["wa"][:].rearrange("p j w -> p w j"))
+        nc.scalar.copy(out=grp_a[:, 1], in_=raw["w0"][:].rearrange("p j w -> p w j"))
         nc.scalar.copy(out=scale[:, D : 2 * D], in_=scale[:, 0:D])
 
-        xb, xc, xs = {}, {}, {}
-        xg, zg, zsrc = {}, {}, {}
-        a_ps, o_ps, l_ps = {}, {}, {}
-        at_sb, z1, mn, ex, sm, rc, gt = {}, {}, {}, {}, {}, {}, {}
+        cp = keep.tile([P, E, R], F32, name="cp")
+        ct = keep.tile([P, E], F32, name="ct")
+        csq1 = keep.tile([P, E], F32, name="csq1")
+        cjunk = keep.tile([P, R], F32, name="cjunk")
+        csq = keep.tile([P, G, E], F32, name="csq")
+        s4 = keep.tile([P, 4], F32, name="s4")
+
+        def prep_c():
+            nc.scalar.copy(out=cp[:], in_=cb[:].rearrange("p (e r) -> p e r", e=E))
+            c_ps = psum.tile([P, E, P], F32, name="turned", bufs=2)
+            for e in range(E):
+                nc.tensor.transpose(c_ps[:, e, :], cp[:, e, :], ident[:])
+            nc.scalar.copy(out=ct[:], in_=c_ps[:, :, 0])
+            for e in range(E):
+                nc.scalar.activation(
+                    out=cjunk[:], in_=cp[:, e, :], func=ACT.Square, scale=0.25, accum_out=csq1[:, e : e + 1]
+                )
+            nc.scalar.copy(out=csq[:], in_=csq1[:].unsqueeze(1).to_broadcast([P, G, E]))
+            nc.scalar.copy(out=s4[:], in_=s_raw[:])
+
+        def prep_r():
+            for t in range(4):
+                nc.scalar.copy(
+                    out=grp_r[:, t],
+                    in_=raw["wa"][:].rearrange("p j (q t) -> p t q j", t=4)[:, t].unsqueeze(1).to_broadcast([P, E, 32, 4]),
+                )
+
+        def prep_b():
+            nc.scalar.copy(out=grp_b[:, 0], in_=raw["wb"][:].rearrange("p j w -> p w j"))
+            nc.scalar.activation(
+                out=grp_b[:, 1], in_=raw["wb"][:].rearrange("p j w -> p w j"), func=ACT.Copy, scale=0.5
+            )
+
+        def quant(codes, scales, src):
+            nc.vector.quantize_mx(out=codes.bitcast(FP8X4), scales=scales, in_=src)
+
+        xb, xg, xc, xs, zg, zc, zsc = {}, {}, {}, {}, {}, {}, {}
+        a_ps, o_ps, l_ps, g_ps = {}, {}, {}, {}
+        at_sb, z1, mn, ex, sm, rc, gpre, gs = {}, {}, {}, {}, {}, {}, {}, {}
+        turned = {}
 
         def widen(g, lo, hi):
             if lo == 0:
                 xb[g] = work.tile([P, G * D], BF16, name="xb", align_bytes=64)
-            w = hi - lo
             nc.vector.tensor_tensor(
-                out=xb[g][:, lo:hi], in0=xbytes[g][:, lo:hi].bitcast(FP8), in1=scale[:, 0:w], op=ALU.mult
+                out=xb[g][:, lo:hi], in0=xbytes[g][:, lo:hi].bitcast(FP8), in1=scale[:, 0 : hi - lo], op=ALU.mult
             )
 
-        def turn(src_words, step, dst, half):
-            bank = psum.tile([P, 2, 2, P], F32, name="turned", bufs=3)
+        def turn(g, half):
+            words = xb[g][:].bitcast(F32)
+            bank = psum.tile([P, 2, 2, P], F32, name="turned", bufs=2)
+            turned[g, half] = bank
             for jj in range(2):
                 base = 256 * (2 * half + jj)
                 for u in range(2):
-                    if step == 2:
-                        cols = src_words[:, base + u : base + 256 : 2]
-                    else:
-                        cols = src_words[:, base + 128 * u : base + 128 * u + 128]
-                    nc.tensor.transpose(bank[:, jj, u, :], cols, ident[:])
-            nc.scalar.copy(
-                out=dst[:, 1024 * half : 1024 * half + 1024].bitcast(F32).rearrange("p (j n u) -> p j n u", j=2, u=2),
-                in_=bank[:].rearrange("p j u n -> p j n u"),
-            )
+                    nc.tensor.transpose(bank[:, jj, u, :], words[:, base + u : base + 256 : 2], ident[:])
 
-        def turn_x(g, half):
+        def exit_x(g, half):
             if half == 0:
                 xg[g] = work.tile([P, 4 * GT], BF16, name="xg", align_bytes=64)
-            turn(xb[g][:].bitcast(F32), 2, xg[g], half)
-
-        def turn_z(g, half):
-            if half == 0:
-                zg[g] = work.tile([P, 4 * GT], BF16, name="zg", align_bytes=64)
-            turn(zsrc[g][:].rearrange("p m k -> p (m k)").bitcast(F32), 1, zg[g], half)
+            nc.scalar.copy(
+                out=xg[g][:, 1024 * half : 1024 * half + 1024].bitcast(F32).rearrange("p (j n u) -> p j n u", j=2, u=2),
+                in_=turned[g, half][:].rearrange("p j u n -> p j n u"),
+            )
 
         def quant_x(g):
-            xc[g] = work.tile([P, GT], U32, name="xc", align_bytes=64)
-            xs[g] = work.tile([P, GT], U8, name="xs", align_bytes=64)
-            nc.vector.quantize_mx(out=xc[g][:].bitcast(FP8X4), scales=xs[g][:], in_=xg[g][:])
-
-        zc, zsc = {}, {}
+            xc[g] = work.tile([P, GT], U32, name="xc", align_bytes=64, bufs=6)
+            xs[g] = work.tile([P, GT], U8, name="xs", align_bytes=64, bufs=6)
+            quant(xc[g][:], xs[g][:], xg[g][:])
 
         def quant_z(g):
             zc[g] = work.tile([P, GT], U32, name="zc", align_bytes=64)
             zsc[g] = work.tile([P, GT], U8, name="zsc", align_bytes=64)
-            nc.vector.quantize_mx(out=zc[g][:].bitcast(FP8X4), scales=zsc[g][:], in_=zg[g][:])
+            quant(zc[g][:], zsc[g][:], zg[g][:])
 
-        def mm(o, lc, ls, rc_, rs, start, stop):
+        def mm(o, lc, ls, rc_, rs, start=True, stop=True):
             nc.tensor.matmul_mx(
                 out=o, lhsT=lc.bitcast(FP8X4), lhsT_scale=ls, rhs=rc_.bitcast(FP8X4), rhs_scale=rs, start=start, stop=stop
             )
 
         def project(g):
             at = psum.tile([P, GT], F32, name="at", bufs=1)
-            mm(at[:], wcode_a[:, 0:P], wscale_a[:, 0:P], xc[g][:], xs[g][:], True, True)
-            a_ps[g] = psum.tile([P, G, R], F32, name="a_ps", bufs=2)
-            for j in range(G):
-                cols = slice(P * j, P * j + P)
-                mm(a_ps[g][:, j, :], xc[g][:, cols], xs[g][:, cols], wcode_a[:, 0:P], wscale_a[:, 0:P], True, True)
+            mm(at[:], wcode_a[:, 0:P], wscale_a[:, 0:P], xc[g][:], xs[g][:])
             at_sb[g] = work.tile([P, GT], F32, name="at_sb")
             nc.scalar.copy(out=at_sb[g][:], in_=at[:])
+
+        def repeat(g, j):
+            a_ps[g, j] = psum.tile([P, 4, P], F32, name="a_ps", bufs=2)
+            cols = slice(P * j, P * j + P)
+            for t in range(4):
+                w = slice(P * t, P * t + P)
+                mm(a_ps[g, j][:, t, :], wcode_r[:, w], wscale_r[:, w], xc[g][:, cols], xs[g][:, cols])
 
         def logits(g):
             l_ps[g] = psum.tile([P, G, E], F32, name="l_ps", bufs=1)
@@ -180,24 +208,34 @@ def tile_hydraloraprototyperouted_t_kernel(tc, x_bytes, x_scale, w0, wa, c, s, w
             nc.vector.reciprocal(out=rc[g][:], in_=sm[g][:])
 
         def soft5(g):
-            gt[g] = work.tile([P, G, E], F32, name="gt")
-            nc.vector.tensor_tensor(
-                out=gt[g][:], in0=ex[g][:], in1=rc[g][:].unsqueeze(2).to_broadcast([P, G, E]), op=ALU.mult
-            )
+            gpre[g] = work.tile([P, G, E, 32], F32, name="gpre")
+            for j in range(G):
+                nc.scalar.activation(
+                    out=gpre[g][:, j], in_=ex[g][:, j, :].unsqueeze(2).to_broadcast([P, E, 32]),
+                    func=ACT.Copy, scale=rc[g][:, j : j + 1],
+                )
+
+        def turn_g(g):
+            g_ps[g] = psum.tile([P, GT], F32, name="g_ps", bufs=1)
+            for j in range(G):
+                nc.tensor.transpose(
+                    g_ps[g][:, P * j : P * j + P], gpre[g][:, j].rearrange("p e q -> p (e q)"), ident[:]
+                )
+
+        def gains(g):
+            gs[g] = work.tile([P, 4, GT], F32, name="gs")
+            for t in range(4):
+                nc.scalar.activation(out=gs[g][:, t, :], in_=g_ps[g][:], func=ACT.Copy, scale=s4[:, t : t + 1])
 
         def mix(g, j):
             if j == 0:
-                zsrc[g] = work.tile([P, G, E * R], BF16, name="zsrc", align_bytes=64)
-            dst = zsrc[g][:, j, :].rearrange("p (u m) -> p u m", u=2)
-            for e in range(E):
-                nc.vector.scalar_tensor_tensor(
-                    out=dst[:, :, 64 * e : 64 * e + 64],
-                    in0=a_ps[g][:, j, :].rearrange("p (u m) -> p u m", u=2),
-                    scalar=gt[g][:, j, e : e + 1],
-                    in1=sp[:, e, :].rearrange("p (u m) -> p u m", u=2),
-                    op0=ALU.mult,
-                    op1=ALU.mult,
-                )
+                zg[g] = work.tile([P, 4 * GT], BF16, name="zg", align_bytes=64)
+            nc.vector.tensor_tensor(
+                out=zg[g][:, 512 * j : 512 * j + 512].rearrange("p (c i t) -> p c t i", i=2, t=4),
+                in0=a_ps[g, j][:].rearrange("p t (c i) -> p c t i", i=2),
+                in1=gs[g][:, :, P * j : P * j + P].rearrange("p t (c i) -> p c t i", i=2),
+                op=ALU.mult,
+            )
 
         def combine(g):
             o_ps[g] = psum.tile([P, G, F], F32, name="o_ps", bufs=1)
@@ -213,100 +251,64 @@ def tile_hydraloraprototyperouted_t_kernel(tc, x_bytes, x_scale, w0, wa, c, s, w
             nc.scalar.copy(out=o_sb[:], in_=o_ps[g][:])
             nc.sync.dma_start(out=out_view[:, G * g : G * g + G, :], in_=o_sb[:])
 
-        widen(0, 0, 512)
-        widen(0, 512, 1024)
-        turn_x(0, 0)
-        nc.scalar.copy(out=grp_a[:, 1], in_=raw["w0"][:].rearrange("p j w -> p w j"))
-        widen(0, 1024, 2048)
-        turn_x(0, 1)
-        nc.vector.quantize_mx(
-            out=wcode_a[:].bitcast(FP8X4), scales=wscale_a[:], in_=grp_a[:].rearrange("p a w j -> p (a w j)")
-        )
-        cp = keep.tile([P, E, R], F32, name="cp")
-        for u in range(2):
-            nc.scalar.copy(
-                out=cp[:, :, 64 * u : 64 * u + 64].rearrange("p e (q i) -> p e q i", i=2),
-                in_=cb[:].rearrange("p (e q u i) -> p u e q i", e=E, u=2, i=2)[:, u],
-            )
-        c_ps = psum.tile([P, E, P], F32, name="turned", bufs=3)
-        for e in range(E):
-            nc.tensor.transpose(c_ps[:, e, :], cp[:, e, :], ident[:])
-        ct = keep.tile([P, E], F32, name="ct")
-        nc.scalar.copy(out=ct[:], in_=c_ps[:, :, 0])
-        csq1 = keep.tile([P, E], F32, name="csq1")
-        cjunk = keep.tile([P, R], F32, name="cjunk")
-        for e in range(E):
-            nc.scalar.activation(
-                out=cjunk[:], in_=cp[:, e, :], func=ACT.Square, scale=0.25, accum_out=csq1[:, e : e + 1]
-            )
-        csq = keep.tile([P, G, E], F32, name="csq")
-        nc.scalar.copy(out=csq[:], in_=csq1[:].unsqueeze(1).to_broadcast([P, G, E]))
+        def ok(g):
+            return 0 <= g < NG
 
-        widen(1, 0, 1024)
-        turn_x(1, 0)
-        widen(1, 1024, 2048)
-        turn_x(1, 1)
-        sp = keep.tile([P, E, R], F32, name="sp")
-        for u in range(2):
-            nc.scalar.copy(
-                out=sp[:, :, 64 * u : 64 * u + 64].rearrange("p e (q i) -> p e q i", i=2),
-                in_=sb[:].rearrange("p (e q u i) -> p u e q i", e=E, u=2, i=2)[:, u],
-            )
-        quant_x(0)
-        project(0)
-        logits(0)
-        widen(2, 0, 1024)
-        turn_x(2, 0)
-        soft1(0)
-        widen(2, 1024, 2048)
-        soft2(0)
-        soft3(0)
-        turn_x(2, 1)
-        nc.scalar.copy(out=grp_b[:, 0], in_=raw["wb"][:].rearrange("p j w -> p w j"))
-        nc.scalar.activation(
-            out=grp_b[:, 1], in_=raw["wb"][:].rearrange("p j w -> p w j"), func=ACT.Copy, scale=0.5
-        )
-        soft4(0)
-        soft5(0)
-
-        for k in range(NG):
-            nxt = k + 1 < NG
-            far = k + 3 < NG
-            if nxt:
-                quant_x(k + 1)
-            if k == 0:
-                nc.vector.quantize_mx(
-                    out=wcode_b[:].bitcast(FP8X4), scales=wscale_b[:], in_=grp_b[:].rearrange("p a w j -> p (a w j)")
-                )
-            if k > 0:
-                combine(k - 1)
-            if nxt:
-                project(k + 1)
-            if k > 0:
+        for k in range(-4, NG):
+            if ok(k + 1):
+                turn_g(k + 1)
+            if ok(k + 2):
+                project(k + 2)
+            if ok(k):
+                mix(k, 0)
+                mix(k, 1)
+                repeat(k, 2)
+                mix(k, 2)
+                repeat(k, 3)
+                mix(k, 3)
+            if ok(k - 1):
                 store(k - 1)
-            if nxt:
-                logits(k + 1)
-            mix(k, 0)
-            mix(k, 1)
-            turn_z(k, 0)
-            mix(k, 2)
-            mix(k, 3)
-            turn_z(k, 1)
-            if nxt:
-                soft1(k + 1)
-            if far:
-                widen(k + 3, 0, 1024)
-            if nxt:
-                soft2(k + 1)
-                soft3(k + 1)
-            if far:
-                turn_x(k + 3, 0)
-                widen(k + 3, 1024, 2048)
-                turn_x(k + 3, 1)
-            if nxt:
-                soft4(k + 1)
-            quant_z(k)
-            if nxt:
-                soft5(k + 1)
-        combine(NG - 1)
+            if ok(k + 1):
+                gains(k + 1)
+            if ok(k + 2):
+                logits(k + 2)
+            if ok(k + 1):
+                repeat(k + 1, 0)
+                repeat(k + 1, 1)
+            if ok(k + 4):
+                if k == -4:
+                    widen(0, 0, 512)
+                    widen(0, 512, 1024)
+                else:
+                    widen(k + 4, 0, 1024)
+                turn(k + 4, 0)
+                exit_x(k + 4, 0)
+            if ok(k + 2):
+                soft1(k + 2)
+            if ok(k):
+                quant_z(k)
+                combine(k)
+            if ok(k + 2):
+                soft2(k + 2)
+                soft3(k + 2)
+            if ok(k + 4):
+                widen(k + 4, 1024, 2048)
+                turn(k + 4, 1)
+            if ok(k + 2):
+                soft4(k + 2)
+                soft5(k + 2)
+            if ok(k + 4):
+                exit_x(k + 4, 1)
+            if k == -4:
+                quant(wcode_a[:], wscale_a[:], grp_a[:].rearrange("p a w j -> p (a w j)"))
+                prep_c()
+            if k == -3:
+                prep_r()
+            if ok(k + 3):
+                quant_x(k + 3)
+            if k == -2:
+                quant(wcode_r[:], wscale_r[:], grp_r[:].rearrange("p t e q j -> p (t e q j)"))
+                prep_b()
+            if k == -1:
+                quant(wcode_b[:], wscale_b[:], grp_b[:].rearrange("p a w j -> p (a w j)"))
         store(NG - 1)

@@ -61,8 +61,8 @@ def tile_hydraloraprototyperouted_t_kernel(tc, x_bytes, x_scale, w0, wa, c, s, w
         load_w("wb", wb)
         cb = keep.tile([P, E * R], BF16, name="cb")
         nc.scalar.dma_start(out=cb[:], in_=c.rearrange("e r -> (e r)").partition_broadcast(P))
-        s_raw = keep.tile([P, 4], BF16, name="s_raw")
-        nc.scalar.dma_start(out=s_raw[:], in_=s.rearrange("(p t) -> p t", t=4))
+        sb = keep.tile([P, E * R], BF16, name="sb")
+        nc.scalar.dma_start(out=sb[:], in_=s.partition_broadcast(P))
         for g in range(2, NG):
             load(g)
 
@@ -73,43 +73,27 @@ def tile_hydraloraprototyperouted_t_kernel(tc, x_bytes, x_scale, w0, wa, c, s, w
 
         grp_a = keep.tile([P, 2, P, 4], BF16, name="grp_a", align_bytes=64)
         grp_b = keep.tile([P, 2, P, 4], BF16, name="grp_b", align_bytes=64)
-        grp_r = keep.tile([P, 4, E, 32, 4], BF16, name="grp_r", align_bytes=64)
         wcode_a = keep.tile([P, 2 * P], U32, name="wcode_a", align_bytes=64)
         wcode_b = keep.tile([P, 2 * P], U32, name="wcode_b", align_bytes=64)
-        wcode_r = keep.tile([P, 4 * P], U32, name="wcode_r", align_bytes=64)
         wscale_a = keep.tile([P, 2 * P], U8, name="wscale_a", align_bytes=64)
         wscale_b = keep.tile([P, 2 * P], U8, name="wscale_b", align_bytes=64)
-        wscale_r = keep.tile([P, 4 * P], U8, name="wscale_r", align_bytes=64)
-        nc.scalar.copy(out=grp_a[:, 0], in_=raw["wa"][:].rearrange("p j w -> p w j"))
-        nc.scalar.copy(out=grp_a[:, 1], in_=raw["w0"][:].rearrange("p j w -> p w j"))
-        nc.scalar.copy(out=scale[:, D : 2 * D], in_=scale[:, 0:D])
-
+        ct = keep.tile([P, 64], F32, name="ct")
+        nc.gpsimd.memset(ct[:], 0.0)
         cp = keep.tile([P, E, R], F32, name="cp")
-        ct = keep.tile([P, E], F32, name="ct")
         csq1 = keep.tile([P, E], F32, name="csq1")
         cjunk = keep.tile([P, R], F32, name="cjunk")
         csq = keep.tile([P, G, E], F32, name="csq")
-        s4 = keep.tile([P, 4], F32, name="s4")
 
-        def prep_c():
-            nc.scalar.copy(out=cp[:], in_=cb[:].rearrange("p (e r) -> p e r", e=E))
-            c_ps = psum.tile([P, E, P], F32, name="turned", bufs=2)
+        def turn_c():
+            c_ps = psum.tile([P, E, P], F32, name="turned", bufs=3)
             for e in range(E):
                 nc.tensor.transpose(c_ps[:, e, :], cp[:, e, :], ident[:])
-            nc.scalar.copy(out=ct[:], in_=c_ps[:, :, 0])
+            nc.scalar.copy(out=ct[:, 0:E], in_=c_ps[:, :, 0])
             for e in range(E):
                 nc.scalar.activation(
                     out=cjunk[:], in_=cp[:, e, :], func=ACT.Square, scale=0.25, accum_out=csq1[:, e : e + 1]
                 )
             nc.scalar.copy(out=csq[:], in_=csq1[:].unsqueeze(1).to_broadcast([P, G, E]))
-            nc.scalar.copy(out=s4[:], in_=s_raw[:])
-
-        def prep_r():
-            for t in range(4):
-                nc.scalar.copy(
-                    out=grp_r[:, t],
-                    in_=raw["wa"][:].rearrange("p j (q t) -> p t q j", t=4)[:, t].unsqueeze(1).to_broadcast([P, E, 32, 4]),
-                )
 
         def prep_b():
             nc.scalar.copy(out=grp_b[:, 0], in_=raw["wb"][:].rearrange("p j w -> p w j"))
@@ -120,195 +104,284 @@ def tile_hydraloraprototyperouted_t_kernel(tc, x_bytes, x_scale, w0, wa, c, s, w
         def quant(codes, scales, src):
             nc.vector.quantize_mx(out=codes.bitcast(FP8X4), scales=scales, in_=src)
 
-        xb, xg, xc, xs, zg, zc, zsc = {}, {}, {}, {}, {}, {}, {}
-        a_ps, o_ps, l_ps, g_ps = {}, {}, {}, {}
-        at_sb, z1, mn, ex, sm, rc, gpre, gs = {}, {}, {}, {}, {}, {}, {}, {}
-        turned = {}
-
-        def widen(g, lo, hi):
-            if lo == 0:
-                xb[g] = work.tile([P, G * D], BF16, name="xb", align_bytes=64)
-            nc.vector.tensor_tensor(
-                out=xb[g][:, lo:hi], in0=xbytes[g][:, lo:hi].bitcast(FP8), in1=scale[:, 0 : hi - lo], op=ALU.mult
+        for u in range(2):
+            nc.scalar.copy(
+                out=grp_a[:, 0, 64 * u : 64 * u + 64, :].rearrange("p (q i) j -> p q i j", i=2),
+                in_=raw["wa"][:].rearrange("p j (q u i) -> p u q i j", u=2, i=2)[:, u],
             )
+        nc.scalar.copy(out=scale[:, D : 2 * D], in_=scale[:, 0:D])
+        nc.scalar.copy(out=grp_a[:, 1], in_=raw["w0"][:].rearrange("p j w -> p w j"))
+        sp = keep.tile([P, E, R], F32, name="sp")
 
-        def turn(g, half):
-            words = xb[g][:].bitcast(F32)
-            bank = psum.tile([P, 2, 2, P], F32, name="turned", bufs=2)
-            turned[g, half] = bank
+        def prep_c():
+            for u in range(2):
+                nc.scalar.copy(
+                    out=cp[:, :, 64 * u : 64 * u + 64].rearrange("p e (q i) -> p e q i", i=2),
+                    in_=cb[:].rearrange("p (e q u i) -> p u e q i", e=E, u=2, i=2)[:, u],
+                )
+            turn_c()
+
+        def prep_s():
+            for u in range(2):
+                nc.scalar.copy(
+                    out=sp[:, :, 64 * u : 64 * u + 64].rearrange("p e (q i) -> p e q i", i=2),
+                    in_=sb[:].rearrange("p (e q u i) -> p u e q i", e=E, u=2, i=2)[:, u],
+                )
+
+        def quant_late():
+            quant(wcode_b[:], wscale_b[:], grp_b[:].rearrange("p a w j -> p (a w j)"))
+
+        held = {}
+
+        def slot(pool, nm, g, shape, dt, bufs, align=None):
+            if (nm, g) not in held:
+                held[nm, g] = pool.tile(shape, dt, name=nm, bufs=bufs, align_bytes=align)
+            return held[nm, g]
+
+        def widen(g, h):
+            xb = slot(work, "xb", g, [P, G * D], BF16, 2, 64)
+            pieces = [(0, 512), (512, 1024)] if (g, h) == (0, 0) else [(1024 * h, 1024 * h + 1024)]
+            for lo, hi in pieces:
+                nc.vector.tensor_tensor(
+                    out=xb[:, lo:hi], in0=xbytes[g][:, lo:hi].bitcast(FP8), in1=scale[:, 0 : hi - lo], op=ALU.mult
+                )
+
+        def turn_x(g, h):
+            words = held["xb", g][:].bitcast(F32)
+            bank = psum.tile([P, 2, 2, P], F32, name="turned", bufs=3)
+            held["tx", g, h] = bank
             for jj in range(2):
-                base = 256 * (2 * half + jj)
+                base = 256 * (2 * h + jj)
                 for u in range(2):
                     nc.tensor.transpose(bank[:, jj, u, :], words[:, base + u : base + 256 : 2], ident[:])
 
-        def exit_x(g, half):
-            if half == 0:
-                xg[g] = work.tile([P, 4 * GT], BF16, name="xg", align_bytes=64)
+        def exit_x(g, h):
+            xg = slot(work, "xg", g, [P, 4 * GT], BF16, 2, 64)
             nc.scalar.copy(
-                out=xg[g][:, 1024 * half : 1024 * half + 1024].bitcast(F32).rearrange("p (j n u) -> p j n u", j=2, u=2),
-                in_=turned[g, half][:].rearrange("p j u n -> p j n u"),
+                out=xg[:, 1024 * h : 1024 * h + 1024].bitcast(F32).rearrange("p (j n u) -> p j n u", j=2, u=2),
+                in_=held["tx", g, h][:].rearrange("p j u n -> p j n u"),
             )
 
         def quant_x(g):
-            xc[g] = work.tile([P, GT], U32, name="xc", align_bytes=64, bufs=6)
-            xs[g] = work.tile([P, GT], U8, name="xs", align_bytes=64, bufs=6)
-            quant(xc[g][:], xs[g][:], xg[g][:])
+            xc = slot(work, "xc", g, [P, GT], U32, 6, 64)
+            xs = slot(work, "xs", g, [P, GT], U8, 6, 64)
+            quant(xc[:], xs[:], held["xg", g][:])
+
+        def mm(o, lc, ls, rc, rs, start=True, stop=True):
+            nc.tensor.matmul_mx(
+                out=o, lhsT=lc.bitcast(FP8X4), lhsT_scale=ls, rhs=rc.bitcast(FP8X4), rhs_scale=rs, start=start, stop=stop
+            )
+
+        def project_t(g):
+            at = slot(psum, "at", g, [P, GT], F32, 1)
+            mm(at[:], wcode_a[:, 0:P], wscale_a[:, 0:P], held["xc", g][:], held["xs", g][:])
+
+        def copy_t(g):
+            at_sb = slot(work, "at_sb", g, [P, GT], F32, 2)
+            nc.scalar.copy(out=at_sb[:], in_=held["at", g][:])
+
+        def logits(g):
+            l_ps = slot(psum, "l_ps", g, [P, G, 64], F32, 1)
+            for j in range(G):
+                nc.tensor.matmul(
+                    l_ps[:, j, :], lhsT=held["at_sb", g][:, P * j : P * j + P], rhs=ct[:], start=True, stop=True
+                )
+
+        def shift(g):
+            z1 = slot(work, "z1", g, [P, G, E], F32, 2)
+            nc.vector.scalar_tensor_tensor(
+                out=z1[:], in0=held["l_ps", g][:, :, 0:E], scalar=-0.125, in1=csq[:], op0=ALU.mult, op1=ALU.add
+            )
+
+        def minimum(g):
+            mn = slot(work, "mn", g, [P, G], F32, 2)
+            nc.vector.tensor_reduce(out=mn[:], in_=held["z1", g][:], axis=AX.X, op=ALU.min)
+
+        def exps(g):
+            ex = slot(work, "ex", g, [P, G, E], F32, 2)
+            sm = slot(work, "sm", g, [P, G], F32, 2)
+            for j in range(G):
+                nc.scalar.activation(
+                    out=ex[:, j, :], in_=held["z1", g][:, j, :], func=ACT.Exp, scale=-1.0,
+                    bias=held["mn", g][:, j : j + 1], accum_out=sm[:, j : j + 1],
+                )
+
+        def recips(g):
+            rc = slot(work, "rc", g, [P, G], F32, 2)
+            nc.vector.reciprocal(out=rc[:], in_=held["sm", g][:])
 
         def quant_z(g):
-            zc[g] = work.tile([P, GT], U32, name="zc", align_bytes=64)
-            zsc[g] = work.tile([P, GT], U8, name="zsc", align_bytes=64)
-            quant(zc[g][:], zsc[g][:], zg[g][:])
+            zc = slot(work, "zc", g, [P, GT], U32, 2, 64)
+            zsc = slot(work, "zsc", g, [P, GT], U8, 2, 64)
+            quant(zc[:], zsc[:], held["zg", g][:])
 
-        def mm(o, lc, ls, rc_, rs, start=True, stop=True):
-            nc.tensor.matmul_mx(
-                out=o, lhsT=lc.bitcast(FP8X4), lhsT_scale=ls, rhs=rc_.bitcast(FP8X4), rhs_scale=rs, start=start, stop=stop
+        def combine(g):
+            o_ps = slot(psum, "o_ps", g, [P, G, F], F32, 1)
+            xc, xs, zc, zsc = held["xc", g], held["xs", g], held["zc", g], held["zsc", g]
+            for j in range(G):
+                cols = slice(P * j, P * j + P)
+                o = o_ps[:, j, :]
+                mm(o, xc[:, cols], xs[:, cols], wcode_a[:, P : 2 * P], wscale_a[:, P : 2 * P], True, False)
+                mm(o, zc[:, cols], zsc[:, cols], wcode_b[:, 0:P], wscale_b[:, 0:P], False, False)
+                mm(o, zc[:, cols], zsc[:, cols], wcode_b[:, P : 2 * P], wscale_b[:, P : 2 * P], False, True)
+
+        def store(g):
+            o_sb = work.tile([P, G, F], F32, name="o_sb", bufs=3)
+            nc.scalar.copy(out=o_sb[:], in_=held["o_ps", g][:])
+            nc.sync.dma_start(out=out_view[:, G * g : G * g + G, :], in_=o_sb[:])
+
+        def gates(g):
+            gt = slot(work, "gt", g, [P, G, E], F32, 2)
+            nc.vector.tensor_tensor(
+                out=gt[:], in0=held["ex", g][:], in1=held["rc", g][:].unsqueeze(2).to_broadcast([P, G, E]), op=ALU.mult
             )
 
         def project(g):
-            at = psum.tile([P, GT], F32, name="at", bufs=1)
-            mm(at[:], wcode_a[:, 0:P], wscale_a[:, 0:P], xc[g][:], xs[g][:])
-            at_sb[g] = work.tile([P, GT], F32, name="at_sb")
-            nc.scalar.copy(out=at_sb[g][:], in_=at[:])
-
-        def repeat(g, j):
-            a_ps[g, j] = psum.tile([P, 4, P], F32, name="a_ps", bufs=2)
-            cols = slice(P * j, P * j + P)
-            for t in range(4):
-                w = slice(P * t, P * t + P)
-                mm(a_ps[g, j][:, t, :], wcode_r[:, w], wscale_r[:, w], xc[g][:, cols], xs[g][:, cols])
-
-        def logits(g):
-            l_ps[g] = psum.tile([P, G, E], F32, name="l_ps", bufs=1)
+            a_ps = slot(psum, "a_ps", g, [P, G, R], F32, 2)
             for j in range(G):
-                nc.tensor.matmul(
-                    l_ps[g][:, j, :], lhsT=at_sb[g][:, P * j : P * j + P], rhs=ct[:], start=True, stop=True
-                )
-
-        def soft1(g):
-            z1[g] = work.tile([P, G, E], F32, name="z1")
-            nc.vector.scalar_tensor_tensor(
-                out=z1[g][:], in0=l_ps[g][:], scalar=-0.125, in1=csq[:], op0=ALU.mult, op1=ALU.add
-            )
-
-        def soft2(g):
-            mn[g] = work.tile([P, G], F32, name="mn")
-            nc.vector.tensor_reduce(out=mn[g][:], in_=z1[g][:], axis=AX.X, op=ALU.min)
-
-        def soft3(g):
-            ex[g] = work.tile([P, G, E], F32, name="ex")
-            sm[g] = work.tile([P, G], F32, name="sm")
-            for j in range(G):
-                nc.scalar.activation(
-                    out=ex[g][:, j, :], in_=z1[g][:, j, :], func=ACT.Exp, scale=-1.0,
-                    bias=mn[g][:, j : j + 1], accum_out=sm[g][:, j : j + 1],
-                )
-
-        def soft4(g):
-            rc[g] = work.tile([P, G], F32, name="rc")
-            nc.vector.reciprocal(out=rc[g][:], in_=sm[g][:])
-
-        def soft5(g):
-            gpre[g] = work.tile([P, G, E, 32], F32, name="gpre")
-            for j in range(G):
-                nc.scalar.activation(
-                    out=gpre[g][:, j], in_=ex[g][:, j, :].unsqueeze(2).to_broadcast([P, E, 32]),
-                    func=ACT.Copy, scale=rc[g][:, j : j + 1],
-                )
-
-        def turn_g(g):
-            g_ps[g] = psum.tile([P, GT], F32, name="g_ps", bufs=1)
-            for j in range(G):
-                nc.tensor.transpose(
-                    g_ps[g][:, P * j : P * j + P], gpre[g][:, j].rearrange("p e q -> p (e q)"), ident[:]
-                )
-
-        def gains(g):
-            gs[g] = work.tile([P, 4, GT], F32, name="gs")
-            for t in range(4):
-                nc.scalar.activation(out=gs[g][:, t, :], in_=g_ps[g][:], func=ACT.Copy, scale=s4[:, t : t + 1])
+                cols = slice(P * j, P * j + P)
+                mm(a_ps[:, j, :], held["xc", g][:, cols], held["xs", g][:, cols], wcode_a[:, 0:P], wscale_a[:, 0:P])
 
         def mix(g, j):
-            if j == 0:
-                zg[g] = work.tile([P, 4 * GT], BF16, name="zg", align_bytes=64)
-            nc.vector.tensor_tensor(
-                out=zg[g][:, 512 * j : 512 * j + 512].rearrange("p (c i t) -> p c t i", i=2, t=4),
-                in0=a_ps[g, j][:].rearrange("p t (c i) -> p c t i", i=2),
-                in1=gs[g][:, :, P * j : P * j + P].rearrange("p t (c i) -> p c t i", i=2),
+            zsrc = slot(work, "zsrc", g, [P, G, E * R], BF16, 2, 64)
+            dst = zsrc[:, j, :].rearrange("p (u m) -> p u m", u=2)
+            for e in range(E):
+                nc.vector.scalar_tensor_tensor(
+                    out=dst[:, :, 64 * e : 64 * e + 64],
+                    in0=held["a_ps", g][:, j, :].rearrange("p (u m) -> p u m", u=2),
+                    scalar=held["gt", g][:, j, e : e + 1],
+                    in1=sp[:, e, :].rearrange("p (u m) -> p u m", u=2),
+                    op0=ALU.mult,
+                    op1=ALU.mult,
+                )
+
+        def weigh(g, j):
+            ag = slot(work, "ag%d" % j, g, [P, E, R], F32, 3)
+            for e in range(E):
+                nc.scalar.activation(
+                    out=ag[:, e, :], in_=held["a_ps", g][:, j, :], func=ACT.Copy, scale=held["gt", g][:, j, e : e + 1]
+                )
+
+        def gain(g, j):
+            zsrc = slot(work, "zsrc", g, [P, G, E * R], BF16, 2, 64)
+            nc.gpsimd.tensor_tensor(
+                out=zsrc[:, j, :].rearrange("p (u e m) -> p e u m", u=2, e=E),
+                in0=held["ag%d" % j, g][:].rearrange("p e (u m) -> p e u m", u=2),
+                in1=sp[:].rearrange("p e (u m) -> p e u m", u=2),
                 op=ALU.mult,
             )
 
-        def combine(g):
-            o_ps[g] = psum.tile([P, G, F], F32, name="o_ps", bufs=1)
-            for j in range(G):
-                cols = slice(P * j, P * j + P)
-                o = o_ps[g][:, j, :]
-                mm(o, xc[g][:, cols], xs[g][:, cols], wcode_a[:, P : 2 * P], wscale_a[:, P : 2 * P], True, False)
-                mm(o, zc[g][:, cols], zsc[g][:, cols], wcode_b[:, 0:P], wscale_b[:, 0:P], False, False)
-                mm(o, zc[g][:, cols], zsc[g][:, cols], wcode_b[:, P : 2 * P], wscale_b[:, P : 2 * P], False, True)
+        def turn_z(g, h):
+            words = held["zsrc", g][:].rearrange("p m k -> p (m k)").bitcast(F32)
+            bank = psum.tile([P, 2, 2, P], F32, name="turned", bufs=3)
+            held["tz", g, h] = bank
+            for jj in range(2):
+                base = 256 * (2 * h + jj)
+                for u in range(2):
+                    nc.tensor.transpose(bank[:, jj, u, :], words[:, base + 128 * u : base + 128 * u + 128], ident[:])
 
-        def store(g):
-            o_sb = work.tile([P, G, F], F32, name="o_sb")
-            nc.scalar.copy(out=o_sb[:], in_=o_ps[g][:])
-            nc.sync.dma_start(out=out_view[:, G * g : G * g + G, :], in_=o_sb[:])
+        def exit_z(g, h):
+            zg = slot(work, "zg", g, [P, 4 * GT], BF16, 2, 64)
+            nc.scalar.copy(
+                out=zg[:, 1024 * h : 1024 * h + 1024].bitcast(F32).rearrange("p (j n u) -> p j n u", j=2, u=2),
+                in_=held["tz", g, h][:].rearrange("p j u n -> p j n u"),
+            )
 
         def ok(g):
             return 0 <= g < NG
 
-        for k in range(-4, NG):
-            if ok(k + 1):
-                turn_g(k + 1)
-            if ok(k + 2):
-                project(k + 2)
-            if ok(k):
-                mix(k, 0)
-                mix(k, 1)
-                repeat(k, 2)
-                mix(k, 2)
-                repeat(k, 3)
-                mix(k, 3)
+        for k in range(NG + 7):
+            if ok(k - 5):
+                g = k - 5
+                mix(g, 1)
+            if ok(k - 5):
+                g = k - 5
+                gain(g, 3)
+            if ok(k - 6):
+                g = k - 6
+                exit_z(g, 1)
             if ok(k - 1):
-                store(k - 1)
-            if ok(k + 1):
-                gains(k + 1)
-            if ok(k + 2):
-                logits(k + 2)
-            if ok(k + 1):
-                repeat(k + 1, 0)
-                repeat(k + 1, 1)
-            if ok(k + 4):
-                if k == -4:
-                    widen(0, 0, 512)
-                    widen(0, 512, 1024)
-                else:
-                    widen(k + 4, 0, 1024)
-                turn(k + 4, 0)
-                exit_x(k + 4, 0)
-            if ok(k + 2):
-                soft1(k + 2)
-            if ok(k):
-                quant_z(k)
-                combine(k)
-            if ok(k + 2):
-                soft2(k + 2)
-                soft3(k + 2)
-            if ok(k + 4):
-                widen(k + 4, 1024, 2048)
-                turn(k + 4, 1)
-            if ok(k + 2):
-                soft4(k + 2)
-                soft5(k + 2)
-            if ok(k + 4):
-                exit_x(k + 4, 1)
-            if k == -4:
-                quant(wcode_a[:], wscale_a[:], grp_a[:].rearrange("p a w j -> p (a w j)"))
-                prep_c()
-            if k == -3:
-                prep_r()
-            if ok(k + 3):
-                quant_x(k + 3)
-            if k == -2:
-                quant(wcode_r[:], wscale_r[:], grp_r[:].rearrange("p t e q j -> p (t e q j)"))
-                prep_b()
-            if k == -1:
-                quant(wcode_b[:], wscale_b[:], grp_b[:].rearrange("p a w j -> p (a w j)"))
-        store(NG - 1)
+                g = k - 1
+                turn_x(g, 0)
+            if ok(k - 4):
+                g = k - 4
+                minimum(g)
+            if ok(k - 5):
+                g = k - 5
+                mix(g, 0)
+            if ok(k - 4):
+                g = k - 4
+                exps(g)
+            if ok(k - 7):
+                g = k - 7
+                combine(g)
+            if ok(k - 5):
+                g = k - 5
+                mix(g, 2)
+            if ok(k - 2):
+                g = k - 2
+                quant_x(g)
+                if g == 2:
+                    quant_late()
+            if ok(k - 1):
+                g = k - 1
+                turn_x(g, 1)
+            if ok(k - 5):
+                g = k - 5
+                turn_z(g, 0)
+            if ok(k - 4):
+                g = k - 4
+                recips(g)
+            if ok(k - 0):
+                g = k - 0
+                widen(g, 0)
+            if ok(k - 1):
+                g = k - 1
+                exit_x(g, 0)
+            if ok(k - 7):
+                g = k - 7
+                store(g)
+            if ok(k - 1):
+                g = k - 1
+                exit_x(g, 1)
+                if g == 0:
+                    prep_c()
+                if g == 1:
+                    prep_s()
+                if g == 2:
+                    prep_b()
+            if ok(k - 3):
+                g = k - 3
+                logits(g)
+            if ok(k - 4):
+                g = k - 4
+                gates(g)
+            if ok(k - 6):
+                g = k - 6
+                quant_z(g)
+            if ok(k - 4):
+                g = k - 4
+                weigh(g, 3)
+            if ok(k - 0):
+                g = k - 0
+                widen(g, 1)
+                if g == 0:
+                    quant(wcode_a[:], wscale_a[:], grp_a[:].rearrange("p a w j -> p (a w j)"))
+            if ok(k - 3):
+                g = k - 3
+                shift(g)
+            if ok(k - 2):
+                g = k - 2
+                project_t(g)
+            if ok(k - 3):
+                g = k - 3
+                project(g)
+            if ok(k - 2):
+                g = k - 2
+                copy_t(g)
+            if ok(k - 5):
+                g = k - 5
+                exit_z(g, 0)
+            if ok(k - 5):
+                g = k - 5
+                turn_z(g, 1)

@@ -37,7 +37,11 @@ def tile_hydraloraprototyperouted_t_kernel(tc, x_bytes, x_scale, w0, wa, c, s, w
         ident = keep.tile([P, P], F32, name="ident")
         make_identity(nc, ident[:])
 
-        scale = keep.tile([P, 2 * D], F32, name="scale")
+        spare = psum.tile([P, P], F32, name="o_ps", bufs=1)
+        for i in range(5):
+            nc.tensor.matmul(spare[:], lhsT=ident[:], rhs=ident[:], start=True, stop=True)
+
+        scale = keep.tile([P, G * D], F32, name="scale")
         nc.scalar.dma_start(out=scale[:, 0:D], in_=x_scale.rearrange("o k -> (o k)").partition_broadcast(P))
         xbytes = {}
 
@@ -81,8 +85,8 @@ def tile_hydraloraprototyperouted_t_kernel(tc, x_bytes, x_scale, w0, wa, c, s, w
         nc.gpsimd.memset(ct[:], 0.0)
         cp = keep.tile([P, E, R], F32, name="cp")
         csq1 = keep.tile([P, E], F32, name="csq1")
-        cjunk = keep.tile([P, R], F32, name="cjunk")
-        csq = keep.tile([P, G, E], F32, name="csq")
+        cjunk = keep.tile([P, E, R], F32, name="cjunk")
+        csq = keep.tile([P, 2 * G, E], F32, name="csq")
 
         def turn_c():
             c_ps = psum.tile([P, E, P], F32, name="turned", bufs=3)
@@ -91,9 +95,9 @@ def tile_hydraloraprototyperouted_t_kernel(tc, x_bytes, x_scale, w0, wa, c, s, w
             nc.scalar.copy(out=ct[:, 0:E], in_=c_ps[:, :, 0])
             for e in range(E):
                 nc.scalar.activation(
-                    out=cjunk[:], in_=cp[:, e, :], func=ACT.Square, scale=0.25, accum_out=csq1[:, e : e + 1]
+                    out=cjunk[:, e, :], in_=cp[:, e, :], func=ACT.Square, scale=0.25, accum_out=csq1[:, e : e + 1]
                 )
-            nc.scalar.copy(out=csq[:], in_=csq1[:].unsqueeze(1).to_broadcast([P, G, E]))
+            nc.scalar.copy(out=csq[:], in_=csq1[:].unsqueeze(1).to_broadcast([P, 2 * G, E]))
 
         def prep_b():
             nc.scalar.copy(out=grp_b[:, 0], in_=raw["wb"][:].rearrange("p j w -> p w j"))
@@ -110,6 +114,7 @@ def tile_hydraloraprototyperouted_t_kernel(tc, x_bytes, x_scale, w0, wa, c, s, w
                 in_=raw["wa"][:].rearrange("p j (q u i) -> p u q i j", u=2, i=2)[:, u],
             )
         nc.scalar.copy(out=scale[:, D : 2 * D], in_=scale[:, 0:D])
+        nc.scalar.copy(out=scale[:, 2 * D : 4 * D], in_=scale[:, 0 : 2 * D])
         nc.scalar.copy(out=grp_a[:, 1], in_=raw["w0"][:].rearrange("p j w -> p w j"))
         sp = keep.tile([P, E, R], F32, name="sp")
 
@@ -132,15 +137,16 @@ def tile_hydraloraprototyperouted_t_kernel(tc, x_bytes, x_scale, w0, wa, c, s, w
             quant(wcode_b[:], wscale_b[:], grp_b[:].rearrange("p a w j -> p (a w j)"))
 
         held = {}
+        PAT = [1,2,1,2,1,2,1,2,1,2,1,2,1,2,1,0]
 
         def slot(pool, nm, g, shape, dt, bufs, align=None):
             if (nm, g) not in held:
                 held[nm, g] = pool.tile(shape, dt, name=nm, bufs=bufs, align_bytes=align)
             return held[nm, g]
 
-        def widen(g, h):
-            xb = slot(work, "xb", g, [P, G * D], BF16, 2, 64)
-            pieces = [(0, 512), (512, 1024)] if (g, h) == (0, 0) else [(1024 * h, 1024 * h + 1024)]
+        def widen(g):
+            xb = slot(work, "xb", g, [P, G * D], BF16, 3, 64)
+            pieces = [(0, 512), (512, 1024), (1024, 2048)] if g == 0 else [(0, 2048)]
             for lo, hi in pieces:
                 nc.vector.tensor_tensor(
                     out=xb[:, lo:hi], in0=xbytes[g][:, lo:hi].bitcast(FP8), in1=scale[:, 0 : hi - lo], op=ALU.mult
@@ -163,8 +169,8 @@ def tile_hydraloraprototyperouted_t_kernel(tc, x_bytes, x_scale, w0, wa, c, s, w
             )
 
         def quant_x(g):
-            xc = slot(work, "xc", g, [P, GT], U32, 6, 64)
-            xs = slot(work, "xs", g, [P, GT], U8, 6, 64)
+            xc = slot(work, "xc", g, [P, GT], U32, 9, 64)
+            xs = slot(work, "xs", g, [P, GT], U8, 9, 64)
             quant(xc[:], xs[:], held["xg", g][:])
 
         def mm(o, lc, ls, rc, rs, start=True, stop=True):
@@ -181,34 +187,41 @@ def tile_hydraloraprototyperouted_t_kernel(tc, x_bytes, x_scale, w0, wa, c, s, w
             nc.scalar.copy(out=at_sb[:], in_=held["at", g][:])
 
         def logits(g):
-            l_ps = slot(psum, "l_ps", g, [P, G, 64], F32, 1)
+            l_ps = slot(psum, "l_ps", g // 2, [P, 2, G, 64], F32, 1)
             for j in range(G):
                 nc.tensor.matmul(
-                    l_ps[:, j, :], lhsT=held["at_sb", g][:, P * j : P * j + P], rhs=ct[:], start=True, stop=True
+                    l_ps[:, g % 2, j, :], lhsT=held["at_sb", g][:, P * j : P * j + P], rhs=ct[:], start=True, stop=True
                 )
 
         def shift(g):
-            z1 = slot(work, "z1", g, [P, G, E], F32, 2)
+            z1 = slot(work, "z1", g // 2, [P, 2 * G, E], F32, 2)
             nc.vector.scalar_tensor_tensor(
-                out=z1[:], in0=held["l_ps", g][:, :, 0:E], scalar=-0.125, in1=csq[:], op0=ALU.mult, op1=ALU.add
+                out=z1[:], in0=held["l_ps", g // 2][:].rearrange("p s j n -> p (s j) n")[:, :, 0:E],
+                scalar=-0.125, in1=csq[:], op0=ALU.mult, op1=ALU.add,
             )
 
         def minimum(g):
-            mn = slot(work, "mn", g, [P, G], F32, 2)
-            nc.vector.tensor_reduce(out=mn[:], in_=held["z1", g][:], axis=AX.X, op=ALU.min)
+            mn = slot(work, "mn", g // 2, [P, 2 * G], F32, 2)
+            nc.vector.tensor_reduce(out=mn[:], in_=held["z1", g // 2][:], axis=AX.X, op=ALU.min)
+
+        def center(g):
+            ce = slot(work, "ce", g // 2, [P, 2 * G, E], F32, 2)
+            nc.gpsimd.tensor_tensor(
+                out=ce[:], in0=held["z1", g // 2][:],
+                in1=held["mn", g // 2][:].unsqueeze(2).to_broadcast([P, 2 * G, E]), op=ALU.subtract,
+            )
 
         def exps(g):
-            ex = slot(work, "ex", g, [P, G, E], F32, 2)
-            sm = slot(work, "sm", g, [P, G], F32, 2)
-            for j in range(G):
-                nc.scalar.activation(
-                    out=ex[:, j, :], in_=held["z1", g][:, j, :], func=ACT.Exp, scale=-1.0,
-                    bias=held["mn", g][:, j : j + 1], accum_out=sm[:, j : j + 1],
-                )
+            ex = slot(work, "ex", g // 2, [P, 2 * G, E], F32, 2)
+            nc.scalar.activation(out=ex[:], in_=held["ce", g // 2][:], func=ACT.Exp, scale=-1.0)
+
+        def total(g):
+            sm = slot(work, "sm", g // 2, [P, 2 * G], F32, 2)
+            nc.vector.tensor_reduce(out=sm[:], in_=held["ex", g // 2][:], axis=AX.X, op=ALU.add)
 
         def recips(g):
-            rc = slot(work, "rc", g, [P, G], F32, 2)
-            nc.vector.reciprocal(out=rc[:], in_=held["sm", g][:])
+            rc = slot(work, "rc", g // 2, [P, 2 * G], F32, 2)
+            nc.vector.reciprocal(out=rc[:], in_=held["sm", g // 2][:])
 
         def quant_z(g):
             zc = slot(work, "zc", g, [P, GT], U32, 2, 64)
@@ -231,10 +244,14 @@ def tile_hydraloraprototyperouted_t_kernel(tc, x_bytes, x_scale, w0, wa, c, s, w
             nc.sync.dma_start(out=out_view[:, G * g : G * g + G, :], in_=o_sb[:])
 
         def gates(g):
-            gt = slot(work, "gt", g, [P, G, E], F32, 2)
-            nc.vector.tensor_tensor(
-                out=gt[:], in0=held["ex", g][:], in1=held["rc", g][:].unsqueeze(2).to_broadcast([P, G, E]), op=ALU.mult
+            gt = slot(work, "gt", g // 2, [P, 2 * G, E], F32, 3)
+            nc.gpsimd.tensor_tensor(
+                out=gt[:], in0=held["ex", g // 2][:],
+                in1=held["rc", g // 2][:].unsqueeze(2).to_broadcast([P, 2 * G, E]), op=ALU.mult,
             )
+
+        def gate(g, j, e):
+            return held["gt", g // 2][:, G * (g % 2) + j, e : e + 1]
 
         def project(g):
             a_ps = slot(psum, "a_ps", g, [P, G, R], F32, 2)
@@ -249,7 +266,7 @@ def tile_hydraloraprototyperouted_t_kernel(tc, x_bytes, x_scale, w0, wa, c, s, w
                 nc.vector.scalar_tensor_tensor(
                     out=dst[:, :, 64 * e : 64 * e + 64],
                     in0=held["a_ps", g][:, j, :].rearrange("p (u m) -> p u m", u=2),
-                    scalar=held["gt", g][:, j, e : e + 1],
+                    scalar=gate(g, j, e),
                     in1=sp[:, e, :].rearrange("p (u m) -> p u m", u=2),
                     op0=ALU.mult,
                     op1=ALU.mult,
@@ -259,7 +276,7 @@ def tile_hydraloraprototyperouted_t_kernel(tc, x_bytes, x_scale, w0, wa, c, s, w
             ag = slot(work, "ag%d" % j, g, [P, E, R], F32, 3)
             for e in range(E):
                 nc.scalar.activation(
-                    out=ag[:, e, :], in_=held["a_ps", g][:, j, :], func=ACT.Copy, scale=held["gt", g][:, j, e : e + 1]
+                    out=ag[:, e, :], in_=held["a_ps", g][:, j, :], func=ACT.Copy, scale=gate(g, j, e)
                 )
 
         def gain(g, j):
@@ -290,59 +307,83 @@ def tile_hydraloraprototyperouted_t_kernel(tc, x_bytes, x_scale, w0, wa, c, s, w
         def ok(g):
             return 0 <= g < NG
 
-        for k in range(NG + 7):
-            if ok(k - 5):
-                g = k - 5
-                mix(g, 1)
-            if ok(k - 5):
-                g = k - 5
-                gain(g, 3)
-            if ok(k - 6):
-                g = k - 6
-                exit_z(g, 1)
-            if ok(k - 1):
-                g = k - 1
-                turn_x(g, 0)
-            if ok(k - 4):
-                g = k - 4
-                minimum(g)
-            if ok(k - 5):
-                g = k - 5
-                mix(g, 0)
-            if ok(k - 4):
-                g = k - 4
-                exps(g)
-            if ok(k - 7):
-                g = k - 7
-                combine(g)
-            if ok(k - 5):
-                g = k - 5
-                mix(g, 2)
+        for k in range(NG + 11):
             if ok(k - 2):
                 g = k - 2
+                turn_x(g, 1)
+            if ok(k - 7) and (k - 7) % 2 == 0:
+                g = k - 7
+                exps(g)
+            if ok(k - 6) and (k - 6) % 2 == 0:
+                g = k - 6
+                shift(g)
+            if ok(k - 8) and PAT[k - 8] >= 1:
+                g = k - 8
+                weigh(g, 3)
+            if ok(k - 7) and (k - 7) % 2 == 0:
+                g = k - 7
+                total(g)
+            if ok(k - 8) and PAT[k - 8] >= 2:
+                g = k - 8
+                weigh(g, 2)
+            if ok(k - 3):
+                g = k - 3
                 quant_x(g)
                 if g == 2:
                     quant_late()
-            if ok(k - 1):
-                g = k - 1
-                turn_x(g, 1)
-            if ok(k - 5):
-                g = k - 5
-                turn_z(g, 0)
-            if ok(k - 4):
-                g = k - 4
-                recips(g)
-            if ok(k - 0):
-                g = k - 0
-                widen(g, 0)
-            if ok(k - 1):
-                g = k - 1
+            if ok(k - 10) and k - 10 < NG - 1:
+                g = k - 10
+                quant_z(g)
+            if ok(k - 2):
+                g = k - 2
                 exit_x(g, 0)
+            if ok(k - 9) and PAT[k - 9] >= 2:
+                g = k - 9
+                gain(g, 2)
+            if ok(k - 6) and (k - 6) % 2 == 0:
+                g = k - 6
+                minimum(g)
+            if ok(k - 11) and k - 11 < NG - 1:
+                g = k - 11
+                store(g)
+            if ok(k - 7) and (k - 7) % 2 == 0:
+                g = k - 7
+                recips(g)
+            if ok(k - 9) and PAT[k - 9] < 1:
+                g = k - 9
+                mix(g, 3)
+            if ok(k - 6) and (k - 6) % 2 == 0:
+                g = k - 6
+                center(g)
+            if ok(k - 9) and k - 9 < NG - 1:
+                g = k - 9
+                turn_z(g, 1)
             if ok(k - 7):
                 g = k - 7
-                store(g)
-            if ok(k - 1):
-                g = k - 1
+                project(g)
+            if ok(k - 9) and k - 9 < NG - 1:
+                g = k - 9
+                exit_z(g, 0)
+            if ok(k - 9) and k - 9 < NG - 1:
+                g = k - 9
+                exit_z(g, 1)
+            if ok(k - 8):
+                g = k - 8
+                mix(g, 1)
+            if ok(k - 8) and PAT[k - 8] >= 1:
+                g = k - 8
+                gain(g, 3)
+            if ok(k - 7) and (k - 7) % 2 == 0:
+                g = k - 7
+                gates(g)
+            if ok(k - 8):
+                g = k - 8
+                mix(g, 0)
+            if ok(k - 8) and PAT[k - 8] < 2:
+                g = k - 8
+                mix(g, 2)
+            if ok(k - 2):
+                g = k - 2
                 exit_x(g, 1)
                 if g == 0:
                     prep_c()
@@ -352,36 +393,55 @@ def tile_hydraloraprototyperouted_t_kernel(tc, x_bytes, x_scale, w0, wa, c, s, w
                     prep_b()
             if ok(k - 3):
                 g = k - 3
+                project_t(g)
+            if ok(k - 4):
+                g = k - 4
                 logits(g)
-            if ok(k - 4):
-                g = k - 4
-                gates(g)
-            if ok(k - 6):
-                g = k - 6
-                quant_z(g)
-            if ok(k - 4):
-                g = k - 4
-                weigh(g, 3)
+            if ok(k - 1):
+                g = k - 1
+                turn_x(g, 0)
+            if ok(k - 3):
+                g = k - 3
+                copy_t(g)
+            if ok(k - 10) and k - 10 < NG - 1:
+                g = k - 10
+                combine(g)
             if ok(k - 0):
                 g = k - 0
-                widen(g, 1)
+                widen(g)
                 if g == 0:
                     quant(wcode_a[:], wscale_a[:], grp_a[:].rearrange("p a w j -> p (a w j)"))
-            if ok(k - 3):
-                g = k - 3
-                shift(g)
-            if ok(k - 2):
-                g = k - 2
-                project_t(g)
-            if ok(k - 3):
-                g = k - 3
-                project(g)
-            if ok(k - 2):
-                g = k - 2
-                copy_t(g)
-            if ok(k - 5):
-                g = k - 5
-                exit_z(g, 0)
-            if ok(k - 5):
-                g = k - 5
-                turn_z(g, 1)
+            if ok(k - 8) and k - 8 < NG - 1:
+                g = k - 8
+                turn_z(g, 0)
+        g = NG - 1
+        quarter, product = {}, {}
+        for j in range(G):
+            words = held["zsrc", g][:, j, :].bitcast(F32)
+            bank = psum.tile([P, 2, P], F32, name="turned", bufs=3)
+            for u in range(2):
+                nc.tensor.transpose(bank[:, u, :], words[:, P * u : P * u + P], ident[:])
+            zg = work.tile([P, P, 4], BF16, name="zg_last", bufs=G, align_bytes=64)
+            nc.scalar.copy(
+                out=zg[:].rearrange("p n t -> p (n t)").bitcast(F32).rearrange("p (n u) -> p n u", u=2),
+                in_=bank[:].rearrange("p u n -> p n u"),
+            )
+            quarter[j] = zg
+        for j in range(G):
+            zc = work.tile([P, P], U32, name="zc_last", bufs=G, align_bytes=64)
+            zsc = work.tile([P, P], U8, name="zsc_last", bufs=G, align_bytes=64)
+            quant(zc[:], zsc[:], quarter[j][:].rearrange("p n t -> p (n t)"))
+            o_ps = psum.tile([P, F], F32, name=("o_ps", "at", "l_ps", "a_ps")[j], bufs=(1, 1, 1, 2)[j])
+            product[j] = o_ps
+            cols = slice(P * j, P * j + P)
+            xc, xs = held["xc", g], held["xs", g]
+            mm(o_ps[:], xc[:, cols], xs[:, cols], wcode_a[:, P : 2 * P], wscale_a[:, P : 2 * P], True, False)
+            mm(o_ps[:], zc[:], zsc[:], wcode_b[:, 0:P], wscale_b[:, 0:P], False, False)
+            mm(o_ps[:], zc[:], zsc[:], wcode_b[:, P : 2 * P], wscale_b[:, P : 2 * P], False, True)
+        for j in range(G):
+            o_sb = work.tile([P, F], F32, name="o_last", bufs=G)
+            if j % 2 == 0:
+                nc.vector.tensor_copy(out=o_sb[:], in_=product[j][:])
+            else:
+                nc.scalar.copy(out=o_sb[:], in_=product[j][:])
+            nc.sync.dma_start(out=out_view[:, G * g + j, :], in_=o_sb[:])

@@ -204,28 +204,22 @@ def tile_hydraloraprototyperouted_t_kernel(tc, x_bytes, x_scale, w0, wa, c, s, w
             mn = slot(work, "mn", g // 2, [P, 2 * G], F32, 2)
             nc.vector.tensor_reduce(out=mn[:], in_=held["z1", g // 2][:], axis=AX.X, op=ALU.min)
 
-        def center(g):
-            ce = slot(work, "ce", g // 2, [P, 2 * G, E], F32, 2)
-            nc.gpsimd.tensor_tensor(
-                out=ce[:], in0=held["z1", g // 2][:],
-                in1=held["mn", g // 2][:].unsqueeze(2).to_broadcast([P, 2 * G, E]), op=ALU.subtract,
-            )
-
         def exps(g):
             ex = slot(work, "ex", g // 2, [P, 2 * G, E], F32, 2)
-            nc.scalar.activation(out=ex[:], in_=held["ce", g // 2][:], func=ACT.Exp, scale=-1.0)
-
-        def total(g):
             sm = slot(work, "sm", g // 2, [P, 2 * G], F32, 2)
-            nc.vector.tensor_reduce(out=sm[:], in_=held["ex", g // 2][:], axis=AX.X, op=ALU.add)
+            for j in range(2 * G):
+                nc.scalar.activation(
+                    out=ex[:, j, :], in_=held["z1", g // 2][:, j, :], func=ACT.Exp, scale=-1.0,
+                    bias=held["mn", g // 2][:, j : j + 1], accum_out=sm[:, j : j + 1],
+                )
 
         def recips(g):
             rc = slot(work, "rc", g // 2, [P, 2 * G], F32, 2)
             nc.vector.reciprocal(out=rc[:], in_=held["sm", g // 2][:])
 
         def quant_z(g):
-            zc = slot(work, "zc", g, [P, GT], U32, 2, 64)
-            zsc = slot(work, "zsc", g, [P, GT], U8, 2, 64)
+            zc = slot(work, "zc", g, [P, GT], U32, 3, 64)
+            zsc = slot(work, "zsc", g, [P, GT], U8, 3, 64)
             quant(zc[:], zsc[:], held["zg", g][:])
 
         def combine(g):
@@ -245,7 +239,7 @@ def tile_hydraloraprototyperouted_t_kernel(tc, x_bytes, x_scale, w0, wa, c, s, w
 
         def gates(g):
             gt = slot(work, "gt", g // 2, [P, 2 * G, E], F32, 3)
-            nc.gpsimd.tensor_tensor(
+            nc.vector.tensor_tensor(
                 out=gt[:], in0=held["ex", g // 2][:],
                 in1=held["rc", g // 2][:].unsqueeze(2).to_broadcast([P, 2 * G, E]), op=ALU.mult,
             )
@@ -260,7 +254,7 @@ def tile_hydraloraprototyperouted_t_kernel(tc, x_bytes, x_scale, w0, wa, c, s, w
                 mm(a_ps[:, j, :], held["xc", g][:, cols], held["xs", g][:, cols], wcode_a[:, 0:P], wscale_a[:, 0:P])
 
         def mix(g, j):
-            zsrc = slot(work, "zsrc", g, [P, G, E * R], BF16, 2, 64)
+            zsrc = slot(work, "zsrc", g, [P, G, E * R], BF16, 3, 64)
             dst = zsrc[:, j, :].rearrange("p (u m) -> p u m", u=2)
             for e in range(E):
                 nc.vector.scalar_tensor_tensor(
@@ -280,7 +274,7 @@ def tile_hydraloraprototyperouted_t_kernel(tc, x_bytes, x_scale, w0, wa, c, s, w
                 )
 
         def gain(g, j):
-            zsrc = slot(work, "zsrc", g, [P, G, E * R], BF16, 2, 64)
+            zsrc = slot(work, "zsrc", g, [P, G, E * R], BF16, 3, 64)
             nc.gpsimd.tensor_tensor(
                 out=zsrc[:, j, :].rearrange("p (u e m) -> p e u m", u=2, e=E),
                 in0=held["ag%d" % j, g][:].rearrange("p e (u m) -> p e u m", u=2),
@@ -307,81 +301,21 @@ def tile_hydraloraprototyperouted_t_kernel(tc, x_bytes, x_scale, w0, wa, c, s, w
         def ok(g):
             return 0 <= g < NG
 
-        for k in range(NG + 11):
-            if ok(k - 2):
-                g = k - 2
-                turn_x(g, 1)
-            if ok(k - 7) and (k - 7) % 2 == 0:
-                g = k - 7
-                exps(g)
-            if ok(k - 6) and (k - 6) % 2 == 0:
-                g = k - 6
-                shift(g)
-            if ok(k - 8) and PAT[k - 8] >= 1:
-                g = k - 8
-                weigh(g, 3)
-            if ok(k - 7) and (k - 7) % 2 == 0:
-                g = k - 7
-                total(g)
-            if ok(k - 8) and PAT[k - 8] >= 2:
-                g = k - 8
-                weigh(g, 2)
-            if ok(k - 3):
-                g = k - 3
-                quant_x(g)
-                if g == 2:
-                    quant_late()
+        for k in range(NG + 10):
+            if ok(k - 9) and k - 9 < NG - 1:
+                g = k - 9
+                quant_z(g)
             if ok(k - 10) and k - 10 < NG - 1:
                 g = k - 10
-                quant_z(g)
-            if ok(k - 2):
-                g = k - 2
-                exit_x(g, 0)
-            if ok(k - 9) and PAT[k - 9] >= 2:
-                g = k - 9
-                gain(g, 2)
-            if ok(k - 6) and (k - 6) % 2 == 0:
-                g = k - 6
-                minimum(g)
-            if ok(k - 11) and k - 11 < NG - 1:
-                g = k - 11
-                store(g)
-            if ok(k - 7) and (k - 7) % 2 == 0:
-                g = k - 7
-                recips(g)
-            if ok(k - 9) and PAT[k - 9] < 1:
-                g = k - 9
-                mix(g, 3)
-            if ok(k - 6) and (k - 6) % 2 == 0:
-                g = k - 6
-                center(g)
-            if ok(k - 9) and k - 9 < NG - 1:
-                g = k - 9
-                turn_z(g, 1)
-            if ok(k - 7):
-                g = k - 7
-                project(g)
-            if ok(k - 9) and k - 9 < NG - 1:
-                g = k - 9
-                exit_z(g, 0)
-            if ok(k - 9) and k - 9 < NG - 1:
-                g = k - 9
-                exit_z(g, 1)
-            if ok(k - 8):
-                g = k - 8
-                mix(g, 1)
+                combine(g)
+            if ok(k - 0):
+                g = k - 0
+                widen(g)
+                if g == 0:
+                    quant(wcode_a[:], wscale_a[:], grp_a[:].rearrange("p a w j -> p (a w j)"))
             if ok(k - 8) and PAT[k - 8] >= 1:
                 g = k - 8
                 gain(g, 3)
-            if ok(k - 7) and (k - 7) % 2 == 0:
-                g = k - 7
-                gates(g)
-            if ok(k - 8):
-                g = k - 8
-                mix(g, 0)
-            if ok(k - 8) and PAT[k - 8] < 2:
-                g = k - 8
-                mix(g, 2)
             if ok(k - 2):
                 g = k - 2
                 exit_x(g, 1)
@@ -391,29 +325,83 @@ def tile_hydraloraprototyperouted_t_kernel(tc, x_bytes, x_scale, w0, wa, c, s, w
                     prep_s()
                 if g == 2:
                     prep_b()
-            if ok(k - 3):
-                g = k - 3
-                project_t(g)
-            if ok(k - 4):
-                g = k - 4
-                logits(g)
+            if ok(k - 6) and (k - 6) % 2 == 0:
+                g = k - 6
+                exps(g)
+            if ok(k - 8) and PAT[k - 8] >= 2:
+                g = k - 8
+                gain(g, 2)
+            if ok(k - 8) and PAT[k - 8] < 1:
+                g = k - 8
+                mix(g, 3)
+            if ok(k - 7) and PAT[k - 7] >= 2:
+                g = k - 7
+                weigh(g, 2)
+            if ok(k - 6) and (k - 6) % 2 == 0:
+                g = k - 6
+                recips(g)
             if ok(k - 1):
                 g = k - 1
                 turn_x(g, 0)
-            if ok(k - 3):
-                g = k - 3
-                copy_t(g)
+            if ok(k - 4):
+                g = k - 4
+                logits(g)
+            if ok(k - 5) and (k - 5) % 2 == 0:
+                g = k - 5
+                shift(g)
+            if ok(k - 7) and PAT[k - 7] < 2:
+                g = k - 7
+                mix(g, 2)
+            if ok(k - 2):
+                g = k - 2
+                quant_x(g)
+                if g == 2:
+                    quant_late()
+            if ok(k - 8) and k - 8 < NG - 1:
+                g = k - 8
+                turn_z(g, 1)
+            if ok(k - 6) and (k - 6) % 2 == 0:
+                g = k - 6
+                gates(g)
             if ok(k - 10) and k - 10 < NG - 1:
                 g = k - 10
-                combine(g)
-            if ok(k - 0):
-                g = k - 0
-                widen(g)
-                if g == 0:
-                    quant(wcode_a[:], wscale_a[:], grp_a[:].rearrange("p a w j -> p (a w j)"))
+                store(g)
             if ok(k - 8) and k - 8 < NG - 1:
                 g = k - 8
                 turn_z(g, 0)
+            if ok(k - 3):
+                g = k - 3
+                project_t(g)
+            if ok(k - 5) and (k - 5) % 2 == 0:
+                g = k - 5
+                minimum(g)
+            if ok(k - 7):
+                g = k - 7
+                mix(g, 0)
+            if ok(k - 6):
+                g = k - 6
+                project(g)
+            if ok(k - 7):
+                g = k - 7
+                mix(g, 1)
+            if ok(k - 1):
+                g = k - 1
+                exit_x(g, 0)
+            if ok(k - 8) and k - 8 < NG - 1:
+                g = k - 8
+                exit_z(g, 1)
+            if ok(k - 3):
+                g = k - 3
+                copy_t(g)
+            if ok(k - 8) and k - 8 < NG - 1:
+                g = k - 8
+                exit_z(g, 0)
+            if ok(k - 6) and PAT[k - 6] >= 1:
+                g = k - 6
+                weigh(g, 3)
+            if ok(k - 1):
+                g = k - 1
+                turn_x(g, 1)
         g = NG - 1
         quarter, product = {}, {}
         for j in range(G):

from contextlib import ExitStack

import concourse.mybir as mybir
from concourse.masks import make_identity

T, D, F, R, E = 8192, 512, 128, 128, 4
P = 128
G = 4
GT = G * P
NG = T // GT
M = T // P
FLOPS = 2 * T * D * (F + R) + 2 * T * E * R * F

F32 = mybir.dt.float32
BF16 = mybir.dt.bfloat16
U32 = mybir.dt.uint32
U8 = mybir.dt.uint8
FP8 = mybir.dt.float8_e4m3fn
FP8X4 = mybir.dt.float8_e4m3fn_x4
ALU = mybir.AluOpType
ACT = mybir.ActivationFunctionType
AX = mybir.AxisListType


def tile_hydraloraprototyperouted_t_kernel(tc, x_bytes, x_scale, w0, wa, c, s, wb, out):
    nc = tc.nc
    x_view = x_bytes.rearrange("(p m) k -> p m k", m=M)
    out_view = out.rearrange("(p m) f -> p m f", m=M)

    with ExitStack() as ctx:
        keep = ctx.enter_context(tc.tile_pool(name="keep", bufs=1))
        byte_pool = ctx.enter_context(tc.tile_pool(name="byte_pool", bufs=NG))
        work = ctx.enter_context(tc.tile_pool(name="work", bufs=3))
        psum = ctx.enter_context(tc.psum_pool(name="psum", bufs=1))
        ctx.enter_context(tc.manual_schedule())

        ident = keep.tile([P, P], F32, name="ident")
        make_identity(nc, ident[:])

        spare = psum.tile([P, P], F32, name="o_ps", bufs=1)
        for i in range(5):
            nc.tensor.matmul(spare[:], lhsT=ident[:], rhs=ident[:], start=True, stop=True)

        scale = keep.tile([P, G * D], F32, name="scale")
        nc.scalar.dma_start(out=scale[:, 0:D], in_=x_scale.rearrange("o k -> (o k)").partition_broadcast(P))
        xbytes = {}

        def load(g):
            xbytes[g] = byte_pool.tile([P, G * D], U8, name="xbytes")
            nc.sync.dma_start(
                out=xbytes[g][:].rearrange("p (m k) -> p m k", m=G),
                in_=x_view[:, G * g : G * g + G, :],
            )

        load(0)
        raw = {}

        def load_w(nm, ap):
            raw[nm] = keep.tile([P, 4, P], BF16, name="raw_" + nm)
            nc.sync.dma_start(out=raw[nm][:], in_=ap.rearrange("(p j) w -> p j w", j=4))

        load_w("wa", wa)
        load_w("w0", w0)
        load(1)
        load_w("wb", wb)
        cb = keep.tile([P, E * R], BF16, name="cb")
        nc.scalar.dma_start(out=cb[:], in_=c.rearrange("e r -> (e r)").partition_broadcast(P))
        sb = keep.tile([P, E * R], BF16, name="sb")
        nc.scalar.dma_start(out=sb[:], in_=s.partition_broadcast(P))
        for g in range(2, NG):
            load(g)

        dummy = keep.tile([P, 1], F32, name="dummy")
        dummy_out = keep.tile([P, 1], F32, name="dummy_out")
        nc.vector.memset(dummy[:], 0.0)
        nc.scalar.activation(out=dummy_out[:], in_=dummy[:], func=ACT.Exp)

        grp_a = keep.tile([P, 2, P, 4], BF16, name="grp_a", align_bytes=64)
        grp_b = keep.tile([P, 2, P, 4], BF16, name="grp_b", align_bytes=64)
        wcode_a = keep.tile([P, 2 * P], U32, name="wcode_a", align_bytes=64)
        wcode_b = keep.tile([P, 2 * P], U32, name="wcode_b", align_bytes=64)
        wscale_a = keep.tile([P, 2 * P], U8, name="wscale_a", align_bytes=64)
        wscale_b = keep.tile([P, 2 * P], U8, name="wscale_b", align_bytes=64)
        ct = keep.tile([P, 64], F32, name="ct")
        nc.gpsimd.memset(ct[:], 0.0)
        cp = keep.tile([P, E, R], F32, name="cp")
        csq1 = keep.tile([P, E], F32, name="csq1")
        cjunk = keep.tile([P, E, R], F32, name="cjunk")
        csq = keep.tile([P, 2 * G, E], F32, name="csq")

        def turn_c():
            c_ps = psum.tile([P, E, P], F32, name="turned", bufs=3)
            for e in range(E):
                nc.tensor.transpose(c_ps[:, e, :], cp[:, e, :], ident[:])
            nc.scalar.copy(out=ct[:, 0:E], in_=c_ps[:, :, 0])
            for e in range(E):
                nc.scalar.activation(
                    out=cjunk[:, e, :], in_=cp[:, e, :], func=ACT.Square, scale=0.25, accum_out=csq1[:, e : e + 1]
                )
            nc.scalar.copy(out=csq[:], in_=csq1[:].unsqueeze(1).to_broadcast([P, 2 * G, E]))

        def prep_b():
            nc.scalar.copy(out=grp_b[:, 0], in_=raw["wb"][:].rearrange("p j w -> p w j"))
            nc.scalar.activation(
                out=grp_b[:, 1], in_=raw["wb"][:].rearrange("p j w -> p w j"), func=ACT.Copy, scale=0.5
            )

        def quant(codes, scales, src):
            nc.vector.quantize_mx(out=codes.bitcast(FP8X4), scales=scales, in_=src)

        for u in range(2):
            nc.scalar.copy(
                out=grp_a[:, 0, 64 * u : 64 * u + 64, :].rearrange("p (q i) j -> p q i j", i=2),
                in_=raw["wa"][:].rearrange("p j (q u i) -> p u q i j", u=2, i=2)[:, u],
            )
        nc.scalar.copy(out=scale[:, D : 2 * D], in_=scale[:, 0:D])
        nc.scalar.copy(out=scale[:, 2 * D : 4 * D], in_=scale[:, 0 : 2 * D])
        nc.scalar.copy(out=grp_a[:, 1], in_=raw["w0"][:].rearrange("p j w -> p w j"))
        sp = keep.tile([P, E, R], F32, name="sp")

        def prep_c():
            for u in range(2):
                nc.scalar.copy(
                    out=cp[:, :, 64 * u : 64 * u + 64].rearrange("p e (q i) -> p e q i", i=2),
                    in_=cb[:].rearrange("p (e q u i) -> p u e q i", e=E, u=2, i=2)[:, u],
                )
            turn_c()

        def prep_s():
            for u in range(2):
                nc.scalar.copy(
                    out=sp[:, :, 64 * u : 64 * u + 64].rearrange("p e (q i) -> p e q i", i=2),
                    in_=sb[:].rearrange("p (e q u i) -> p u e q i", e=E, u=2, i=2)[:, u],
                )

        def quant_late():
            quant(wcode_b[:], wscale_b[:], grp_b[:].rearrange("p a w j -> p (a w j)"))

        held = {}
        PAT = [1,2,1,2,1,2,1,2,1,2,1,2,1,2,1,0]

        def slot(pool, nm, g, shape, dt, bufs, align=None):
            if (nm, g) not in held:
                held[nm, g] = pool.tile(shape, dt, name=nm, bufs=bufs, align_bytes=align)
            return held[nm, g]

        def widen(g):
            xb = slot(work, "xb", g, [P, G * D], BF16, 3, 64)
            pieces = [(0, 512), (512, 1024), (1024, 2048)] if g == 0 else [(0, 2048)]
            for lo, hi in pieces:
                nc.vector.tensor_tensor(
                    out=xb[:, lo:hi], in0=xbytes[g][:, lo:hi].bitcast(FP8), in1=scale[:, 0 : hi - lo], op=ALU.mult
                )

        def turn_x(g, h):
            words = held["xb", g][:].bitcast(F32)
            bank = psum.tile([P, 2, 2, P], F32, name="turned", bufs=3)
            held["tx", g, h] = bank
            for jj in range(2):
                base = 256 * (2 * h + jj)
                for u in range(2):
                    nc.tensor.transpose(bank[:, jj, u, :], words[:, base + u : base + 256 : 2], ident[:])

        def exit_x(g, h):
            xg = slot(work, "xg", g, [P, 4 * GT], BF16, 2, 64)
            nc.scalar.copy(
                out=xg[:, 1024 * h : 1024 * h + 1024].bitcast(F32).rearrange("p (j n u) -> p j n u", j=2, u=2),
                in_=held["tx", g, h][:].rearrange("p j u n -> p j n u"),
            )

        def quant_x(g):
            xc = slot(work, "xc", g, [P, GT], U32, 9, 64)
            xs = slot(work, "xs", g, [P, GT], U8, 9, 64)
            quant(xc[:], xs[:], held["xg", g][:])

        def mm(o, lc, ls, rc, rs, start=True, stop=True):
            nc.tensor.matmul_mx(
                out=o, lhsT=lc.bitcast(FP8X4), lhsT_scale=ls, rhs=rc.bitcast(FP8X4), rhs_scale=rs, start=start, stop=stop
            )

        def project_t(g):
            at = slot(psum, "at", g, [P, GT], F32, 1)
            mm(at[:], wcode_a[:, 0:P], wscale_a[:, 0:P], held["xc", g][:], held["xs", g][:])

        def copy_t(g):
            at_sb = slot(work, "at_sb", g, [P, GT], F32, 2)
            nc.scalar.copy(out=at_sb[:], in_=held["at", g][:])

        def logits(g):
            l_ps = slot(psum, "l_ps", g // 2, [P, 2, G, 64], F32, 1)
            for j in range(G):
                nc.tensor.matmul(
                    l_ps[:, g % 2, j, :], lhsT=held["at_sb", g][:, P * j : P * j + P], rhs=ct[:], start=True, stop=True
                )

        def shift(g):
            z1 = slot(work, "z1", g // 2, [P, 2 * G, E], F32, 2)
            nc.vector.scalar_tensor_tensor(
                out=z1[:], in0=held["l_ps", g // 2][:].rearrange("p s j n -> p (s j) n")[:, :, 0:E],
                scalar=-0.125, in1=csq[:], op0=ALU.mult, op1=ALU.add,
            )

        def minimum(g):
            mn = slot(work, "mn", g // 2, [P, 2 * G], F32, 2)
            nc.vector.tensor_reduce(out=mn[:], in_=held["z1", g // 2][:], axis=AX.X, op=ALU.min)

        def exps(g):
            ex = slot(work, "ex", g // 2, [P, 2 * G, E], F32, 2)
            sm = slot(work, "sm", g // 2, [P, 2 * G], F32, 2)
            for j in range(2 * G):
                nc.scalar.activation(
                    out=ex[:, j, :], in_=held["z1", g // 2][:, j, :], func=ACT.Exp, scale=-1.0,
                    bias=held["mn", g // 2][:, j : j + 1], accum_out=sm[:, j : j + 1],
                )

        def recips(g):
            rc = slot(work, "rc", g // 2, [P, 2 * G], F32, 2)
            nc.vector.reciprocal(out=rc[:], in_=held["sm", g // 2][:])

        def quant_z(g):
            zc = slot(work, "zc", g, [P, GT], U32, 3, 64)
            zsc = slot(work, "zsc", g, [P, GT], U8, 3, 64)
            quant(zc[:], zsc[:], held["zg", g][:])

        def combine(g):
            o_ps = slot(psum, "o_ps", g, [P, G, F], F32, 1)
            xc, xs, zc, zsc = held["xc", g], held["xs", g], held["zc", g], held["zsc", g]
            for j in range(G):
                cols = slice(P * j, P * j + P)
                o = o_ps[:, j, :]
                mm(o, xc[:, cols], xs[:, cols], wcode_a[:, P : 2 * P], wscale_a[:, P : 2 * P], True, False)
                mm(o, zc[:, cols], zsc[:, cols], wcode_b[:, 0:P], wscale_b[:, 0:P], False, False)
                mm(o, zc[:, cols], zsc[:, cols], wcode_b[:, P : 2 * P], wscale_b[:, P : 2 * P], False, True)

        def store(g):
            o_sb = work.tile([P, G, F], F32, name="o_sb", bufs=3)
            nc.scalar.copy(out=o_sb[:], in_=held["o_ps", g][:])
            nc.sync.dma_start(out=out_view[:, G * g : G * g + G, :], in_=o_sb[:])

        def gates(g):
            gt = slot(work, "gt", g // 2, [P, 2 * G, E], F32, 3)
            nc.vector.tensor_tensor(
                out=gt[:], in0=held["ex", g // 2][:],
                in1=held["rc", g // 2][:].unsqueeze(2).to_broadcast([P, 2 * G, E]), op=ALU.mult,
            )

        def gate(g, j, e):
            return held["gt", g // 2][:, G * (g % 2) + j, e : e + 1]

        def project(g):
            a_ps = slot(psum, "a_ps", g, [P, G, R], F32, 2)
            for j in range(G):
                cols = slice(P * j, P * j + P)
                mm(a_ps[:, j, :], held["xc", g][:, cols], held["xs", g][:, cols], wcode_a[:, 0:P], wscale_a[:, 0:P])

        def mix(g, j):
            zsrc = slot(work, "zsrc", g, [P, G, E * R], BF16, 3, 64)
            dst = zsrc[:, j, :].rearrange("p (u m) -> p u m", u=2)
            for e in range(E):
                nc.vector.scalar_tensor_tensor(
                    out=dst[:, :, 64 * e : 64 * e + 64],
                    in0=held["a_ps", g][:, j, :].rearrange("p (u m) -> p u m", u=2),
                    scalar=gate(g, j, e),
                    in1=sp[:, e, :].rearrange("p (u m) -> p u m", u=2),
                    op0=ALU.mult,
                    op1=ALU.mult,
                )

        def weigh(g, j):
            ag = slot(work, "ag%d" % j, g, [P, E, R], F32, 3)
            for e in range(E):
                nc.scalar.activation(
                    out=ag[:, e, :], in_=held["a_ps", g][:, j, :], func=ACT.Copy, scale=gate(g, j, e)
                )

        def gain(g, j):
            zsrc = slot(work, "zsrc", g, [P, G, E * R], BF16, 3, 64)
            nc.gpsimd.tensor_tensor(
                out=zsrc[:, j, :].rearrange("p (u e m) -> p e u m", u=2, e=E),
                in0=held["ag%d" % j, g][:].rearrange("p e (u m) -> p e u m", u=2),
                in1=sp[:].rearrange("p e (u m) -> p e u m", u=2),
                op=ALU.mult,
            )

        def turn_z(g, h):
            words = held["zsrc", g][:].rearrange("p m k -> p (m k)").bitcast(F32)
            bank = psum.tile([P, 2, 2, P], F32, name="turned", bufs=3)
            held["tz", g, h] = bank
            for jj in range(2):
                base = 256 * (2 * h + jj)
                for u in range(2):
                    nc.tensor.transpose(bank[:, jj, u, :], words[:, base + 128 * u : base + 128 * u + 128], ident[:])

        def exit_z(g, h):
            zg = slot(work, "zg", g, [P, 4 * GT], BF16, 2, 64)
            nc.scalar.copy(
                out=zg[:, 1024 * h : 1024 * h + 1024].bitcast(F32).rearrange("p (j n u) -> p j n u", j=2, u=2),
                in_=held["tz", g, h][:].rearrange("p j u n -> p j n u"),
            )

        def ok(g):
            return 0 <= g < NG

        for k in range(NG + 10):
            if ok(k - 9) and k - 9 < NG - 1:
                g = k - 9
                quant_z(g)
            if ok(k - 10) and k - 10 < NG - 1:
                g = k - 10
                combine(g)
            if ok(k - 0):
                g = k - 0
                widen(g)
                if g == 0:
                    quant(wcode_a[:], wscale_a[:], grp_a[:].rearrange("p a w j -> p (a w j)"))
            if ok(k - 8) and PAT[k - 8] >= 1:
                g = k - 8
                gain(g, 3)
            if ok(k - 2):
                g = k - 2
                exit_x(g, 1)
                if g == 0:
                    prep_c()
                if g == 1:
                    prep_s()
                if g == 2:
                    prep_b()
            if ok(k - 6) and (k - 6) % 2 == 0:
                g = k - 6
                exps(g)
            if ok(k - 8) and PAT[k - 8] >= 2:
                g = k - 8
                gain(g, 2)
            if ok(k - 8) and PAT[k - 8] < 1:
                g = k - 8
                mix(g, 3)
            if ok(k - 7) and PAT[k - 7] >= 2:
                g = k - 7
                weigh(g, 2)
            if ok(k - 6) and (k - 6) % 2 == 0:
                g = k - 6
                recips(g)
            if ok(k - 1):
                g = k - 1
                turn_x(g, 0)
            if ok(k - 4):
                g = k - 4
                logits(g)
            if ok(k - 5) and (k - 5) % 2 == 0:
                g = k - 5
                shift(g)
            if ok(k - 7) and PAT[k - 7] < 2:
                g = k - 7
                mix(g, 2)
            if ok(k - 2):
                g = k - 2
                quant_x(g)
                if g == 2:
                    quant_late()
            if ok(k - 8) and k - 8 < NG - 1:
                g = k - 8
                turn_z(g, 1)
            if ok(k - 6) and (k - 6) % 2 == 0:
                g = k - 6
                gates(g)
            if ok(k - 10) and k - 10 < NG - 1:
                g = k - 10
                store(g)
            if ok(k - 8) and k - 8 < NG - 1:
                g = k - 8
                turn_z(g, 0)
            if ok(k - 3):
                g = k - 3
                project_t(g)
            if ok(k - 5) and (k - 5) % 2 == 0:
                g = k - 5
                minimum(g)
            if ok(k - 7):
                g = k - 7
                mix(g, 0)
            if ok(k - 6):
                g = k - 6
                project(g)
            if ok(k - 7):
                g = k - 7
                mix(g, 1)
            if ok(k - 1):
                g = k - 1
                exit_x(g, 0)
            if ok(k - 8) and k - 8 < NG - 1:
                g = k - 8
                exit_z(g, 1)
            if ok(k - 3):
                g = k - 3
                copy_t(g)
            if ok(k - 8) and k - 8 < NG - 1:
                g = k - 8
                exit_z(g, 0)
            if ok(k - 6) and PAT[k - 6] >= 1:
                g = k - 6
                weigh(g, 3)
            if ok(k - 1):
                g = k - 1
                turn_x(g, 1)
        g = NG - 1
        quarter, product = {}, {}
        for j in range(G):
            words = held["zsrc", g][:, j, :].bitcast(F32)
            bank = psum.tile([P, 2, P], F32, name="turned", bufs=3)
            for u in range(2):
                nc.tensor.transpose(bank[:, u, :], words[:, P * u : P * u + P], ident[:])
            zg = work.tile([P, P, 4], BF16, name="zg_last", bufs=G, align_bytes=64)
            nc.scalar.copy(
                out=zg[:].rearrange("p n t -> p (n t)").bitcast(F32).rearrange("p (n u) -> p n u", u=2),
                in_=bank[:].rearrange("p u n -> p n u"),
            )
            quarter[j] = zg
        for j in range(G):
            zc = work.tile([P, P], U32, name="zc_last", bufs=G, align_bytes=64)
            zsc = work.tile([P, P], U8, name="zsc_last", bufs=G, align_bytes=64)
            quant(zc[:], zsc[:], quarter[j][:].rearrange("p n t -> p (n t)"))
            o_ps = psum.tile([P, F], F32, name=("o_ps", "at", "l_ps", "a_ps")[j], bufs=(1, 1, 1, 2)[j])
            product[j] = o_ps
            cols = slice(P * j, P * j + P)
            xc, xs = held["xc", g], held["xs", g]
            mm(o_ps[:], xc[:, cols], xs[:, cols], wcode_a[:, P : 2 * P], wscale_a[:, P : 2 * P], True, False)
            mm(o_ps[:], zc[:], zsc[:], wcode_b[:, 0:P], wscale_b[:, 0:P], False, False)
            mm(o_ps[:], zc[:], zsc[:], wcode_b[:, P : 2 * P], wscale_b[:, P : 2 * P], False, True)
        for j in range(G):
            o_sb = work.tile([P, F], F32, name="o_last", bufs=G)
            if j % 2 == 0:
                nc.vector.tensor_copy(out=o_sb[:], in_=product[j][:])
            else:
                nc.scalar.copy(out=o_sb[:], in_=product[j][:])
            nc.sync.dma_start(out=out_view[:, G * g + j, :], in_=o_sb[:])
